import numpy as np
import ml_dtypes


def mxq(x, axis, fmt="e4m3"):
    dtype, down = {"e4m3": (ml_dtypes.float8_e4m3fn, 7), "e5m2": (ml_dtypes.float8_e5m2, 14)}[fmt]
    v = np.moveaxis(np.asarray(x, np.float32).astype(ml_dtypes.bfloat16).astype(np.float64), axis, -1)
    blocks = v.reshape(v.shape[:-1] + (-1, 32))
    amax = np.abs(blocks).max(-1, keepdims=True)
    byte = np.maximum(np.where(amax > 0, np.frexp(amax)[1] - 1 + 127, 0) - down, 1)
    scale = np.exp2(byte - 127.0)
    codes = (blocks / scale).astype(np.float32).astype(dtype).astype(np.float64)
    return np.moveaxis((codes * scale).reshape(v.shape), -1, axis)


WIDE = False


def mx_kscale(k):
    if not WIDE:
        return np.ones(k)
    levels = np.array([10, -10, 5, -5, 0])
    if k % 512:
        return np.exp2(np.random.permutation(np.resize(levels, k // 32))).repeat(32)
    a = np.empty((k // 512, 16))
    for p in range(k // 512):
        a[p, :8] = np.random.permutation(np.resize(levels, 8))
        for g in range(8):
            far = levels[np.abs(levels - a[p, g]) >= 10]
            a[p, g + 8] = far[np.random.randint(len(far))]
    return np.exp2(a.ravel()).repeat(32)


def f64(x):
    return np.asarray(x).astype(np.float64)


def striped(idx):
    return np.tile(idx.reshape(-1, 16).T, (8, 1)).astype(np.uint16)


def unstriped(offs):
    return offs[:16].T.reshape(-1).astype(np.int64)


E2M1 = np.array([0.0, 0.5, 1.0, 1.5, 2.0, 3.0, 4.0, 6.0, -0.0, -0.5, -1.0, -1.5, -2.0, -3.0, -4.0, -6.0])


def pack_weight(w, fmt):
    k, n = w.shape
    w = f64(np.asarray(w, np.float32).astype(ml_dtypes.bfloat16)).reshape(k // 32, 32, n)
    amax = np.abs(w).max(1)
    if fmt == "e4m3":
        byte = np.frexp(amax)[1] - 1 + 127 - 7
    else:
        mant, ex = np.frexp(amax / 6.0)
        byte = np.where(mant > 0.5, ex, ex - 1) + 127
    byte = np.clip(np.where(amax > 0, byte, 1), 1, 254)
    scaled = (w * np.exp2(127.0 - byte)[:, None, :]).reshape(k, n).astype(np.float32)
    by_word = np.ascontiguousarray(scaled.reshape(k // 512, 128, 4, n).transpose(0, 1, 3, 2))
    if fmt == "e4m3":
        words = by_word.astype(ml_dtypes.float8_e4m3fn).view(np.uint8)
    else:
        c = by_word.astype(ml_dtypes.float4_e2m1fn).view(np.uint8) & 0xF
        words = (c[..., 0::2] | (c[..., 1::2] << 4)).reshape(k // 512, 128, 2 * n)
    return np.ascontiguousarray(words), np.ascontiguousarray(byte.astype(np.uint8).reshape(k // 512, 16, n))


def unpack_weight(words, scales, fmt):
    g, _, n = scales.shape
    words = np.ascontiguousarray(words).reshape(g, 128, n, -1)
    if fmt == "e4m3":
        vals = words.view(ml_dtypes.float8_e4m3fn).astype(np.float64)
    else:
        nib = np.empty((g, 128, n, 4), np.uint8)
        nib[..., 0::2] = words & 0xF
        nib[..., 1::2] = words >> 4
        vals = E2M1[nib]
    vals = vals * np.repeat(np.exp2(scales.astype(np.float64) - 127.0), 8, axis=1)[..., None]
    return vals.transpose(0, 1, 3, 2).reshape(g * 512, n)


def gelu(v):
    return 0.5 * v * (1.0 + np.tanh(np.sqrt(2.0 / np.pi) * (v + 0.044715 * v**3)))


K, T, S, H, T2, P = 1024, 2048, 512, 1024, 1024, 512


def setup_inputs():
    n = np.random.standard_normal
    s = mx_kscale(K)[:, None]
    u = mx_kscale(H)[:, None]
    tab_words, tab_scales = pack_weight(n((K, T)) * s, "e4m3")
    w4_words, w4_scales = pack_weight(0.8 * n((K, H)) / np.sqrt(K) / s, "e2m1")
    return {
        "tab_words": tab_words, "tab_scales": tab_scales,
        "offs": striped(np.random.permutation(T)[:S]),
        "w4_words": w4_words, "w4_scales": w4_scales,
        "w1": (0.8 * n((K, H)) / np.sqrt(K) / s).astype(np.float32),
        "w3": (1.1 * n((K, H)) / np.sqrt(K) / s).astype(np.float32),
        "gain": (1.2 * np.exp(0.3 * n(H)) * u[:, 0]).astype(np.float32),
        "page0": (n((H, T2)) * u).astype(np.float32),
        "wgs": np.exp(0.3 * n((128, S))).astype(np.float32),
        "offs2": striped(np.random.permutation(T2)[:S]),
        "offs3": striped(np.random.permutation(T2)[:P]),
        "offs4": striped(np.random.permutation(T2)[:P]),
        "dv": (n(H) / np.sqrt(H) / u[:, 0] ** 2).astype(np.float32),
        "fv": n(P).astype(np.float32),
        "jv": np.exp(0.3 * n(P)).astype(np.float32),
    }


def reference(tab_words, tab_scales, offs, w4_words, w4_scales, w1, w3, gain, page0, wgs, offs2, offs3, offs4, dv, fv, jv):
    v = unpack_weight(tab_words, tab_scales, "e4m3")[:, unstriped(offs)]
    w4 = unpack_weight(w4_words, w4_scales, "e2m1")
    b = w4.T @ v + mxq(f64(w1), 0, "e4m3").T @ v
    d = mxq(f64(w3), 0, "e4m3").T @ v
    h = f64(gain)[:, None] * np.tanh(np.maximum(b, d))
    page = f64(page0).copy()
    page[:, unstriped(offs2)] = np.tile(f64(wgs), (H // 128, 1)) * h
    x1 = page[:, unstriped(offs3)]
    x2 = np.abs(page[:, unstriped(offs4)]) * f64(dv)[:, None]
    e = mxq(x1, 0, "e4m3").T @ mxq(x2, 0, "e4m3")
    return (e + f64(fv)[:, None]) * f64(jv)[None, :]

@@ -1,0 +1,370 @@
+from contextlib import ExitStack
+
+import concourse.mybir as mybir
+from concourse.masks import make_identity
+
+K, T, S, H, T2, NP = 1024, 2048, 512, 1024, 1024, 512
+FLOPS = 2 * (3 * K * H * S + H * NP * NP)
+
+F32 = mybir.dt.float32
+BF16 = mybir.dt.bfloat16
+I32 = mybir.dt.int32
+U32 = mybir.dt.uint32
+U16 = mybir.dt.uint16
+U8 = mybir.dt.uint8
+FP8X4 = mybir.dt.float8_e4m3fn_x4
+FP4X4 = mybir.dt.float4_e2m1fn_x4
+ALU = mybir.AluOpType
+ACT = mybir.ActivationFunctionType
+
+P = 128
+PACK = 4
+PASSES = 2
+TILES = 8
+HALF = 4
+
+
+def tile_list_braze_wetting_scores_kernel(
+    tc, tab_words, tab_scales, offs, w4_words, w4_scales, w1, w3, gain, page0, wgs, offs2, offs3, offs4, dv, fv, jv, out
+):
+    nc = tc.nc
+    with ExitStack() as ctx:
+        lists = ctx.enter_context(tc.tile_pool(name="lists", bufs=1))
+        keep = ctx.enter_context(tc.tile_pool(name="keep", bufs=1))
+        psum = ctx.enter_context(tc.psum_pool(name="psum", bufs=1))
+
+        def held(name, shape, dtype):
+            return keep.tile(shape, dtype, name=name, align_bytes=64)
+
+        def shared(name, shape, dtype, tag, bufs):
+            return keep.tile(shape, dtype, name=name, tag=tag, bufs=bufs, align_bytes=64)
+
+        banks = [psum.tile([P, 512], F32, name=f"bank{n}") for n in range(8)]
+        weights = (w1, w3)
+
+        tab_planes = held("tab_planes", [P, PASSES, T], U8)
+        w4_planes = held("w4_planes", [P, PASSES, H], U8)
+        vec_rows = shared("vec_rows", [P, P], F32, "gate_d", 1)
+        nc.vector.memset(tab_planes[:].bitcast(I32), 0)
+        nc.vector.memset(vec_rows[:], 0.0)
+        nc.vector.memset(w4_planes[:].bitcast(I32), 0)
+
+        idx = lists.tile([P, S // 16], U16, name="idx")
+        idx2 = lists.tile([P, S // 16], U16, name="idx2")
+        idx3 = lists.tile([P, NP // 16], U16, name="idx3")
+        idx4 = lists.tile([P, NP // 16], U16, name="idx4")
+
+        raw = {}
+
+        def load_natural_weights(u, which=(1, 0)):
+            for w in which:
+                for a in range(PASSES):
+                    if u >= 2 and w == 0:
+                        raw[u, w, a] = held(f"raw{u}{w}{a}", [P, PACK, P], F32)
+                    else:
+                        raw[u, w, a] = shared(f"raw{u}{w}{a}", [P, PACK, P], F32, "small", 12)
+                    rows = weights[w][512 * a : 512 * (a + 1), P * u : P * (u + 1)]
+                    nc.sync.dma_start(out=raw[u, w, a][:], in_=rows.rearrange("(p j) c -> p j c", j=PACK))
+
+        pages = {}
+
+        def load_page(u):
+            pages[u] = shared(f"page{u}", [P, T2], F32, f"page{u}", 1)
+            if u < HALF:
+                nc.sync.dma_start(out=pages[u][:], in_=page0[P * u : P * (u + 1), :])
+            else:
+                rows = page0[512:, :].rearrange("(q t i) c -> t q i c", t=PACK, i=8)
+                nc.sync.dma_start(out=pages[u][:], in_=rows[u - HALF])
+
+        def load_scales(queue, planes, src):
+            for quad in range(4):
+                queue.dma_start(
+                    out=planes[32 * quad : 32 * quad + 4].bitcast(I32),
+                    in_=src[:, 4 * quad : 4 * quad + 4, :].rearrange("a r c -> r a c").bitcast(I32),
+                )
+
+        nc.sync.dma_start(idx[:], offs)
+        tab = [shared(f"tab{a}", [P, T], U32, "large", 2) for a in range(PASSES)]
+
+        def load_table(a):
+            nc.sync.dma_start(out=tab[a][:].bitcast(I32), in_=tab_words[a].rearrange("p t i -> p (t i)").bitcast(I32))
+
+        load_natural_weights(0, (1,))
+        load_table(0)
+        load_natural_weights(0, (0,))
+        load_scales(nc.sync, tab_planes, tab_scales)
+        load_table(1)
+        w4_halves = [held(f"w4_half{n}", [P, PASSES, 1024], U8) for n in range(2)]
+
+        def load_w4(n):
+            src = w4_words[:, :, 1024 * n : 1024 * (n + 1)].rearrange("a p c -> p a c")
+            nc.sync.dma_start(out=w4_halves[n][:].bitcast(I32), in_=src.bitcast(I32))
+
+        load_w4(0)
+
+        load_scales(nc.gpsimd, w4_planes, w4_scales)
+        gain_first = held("gain_first", [P, HALF], F32)
+        with nc.allow_non_contiguous_dma(reason="one gain a partition"):
+            nc.sync.dma_start(out=gain_first[:], in_=gain[0:512].rearrange("(u p) -> p u", p=P))
+        wgs_nat = held("wgs_nat", [P, S], F32)
+        nc.sync.dma_start(out=wgs_nat[:], in_=wgs)
+        load_natural_weights(1)
+        load_page(0)
+        nc.sync.dma_start(idx2[:], offs2)
+        nc.sync.dma_start(idx4[:], offs4)
+        nc.sync.dma_start(idx3[:], offs3)
+        load_natural_weights(2)
+        load_page(1)
+        load_natural_weights(3)
+        wide = {}
+
+        def load_wide(w, a):
+            wide[w, a] = held(f"wide{w}{a}", [P, PACK, 512], F32)
+            rows = weights[w][512 * a : 512 * (a + 1), 512:]
+            nc.sync.dma_start(out=wide[w, a][:], in_=rows.rearrange("(p j) c -> p j c", j=PACK))
+
+        load_wide(1, 0)
+        load_wide(1, 1)
+        load_page(2)
+        load_wide(0, 0)
+        load_wide(0, 1)
+        nc.sync.dma_start(out=vec_rows[8:12, :], in_=dv[0:512].rearrange("(u p) -> u p", p=P))
+        for row, vec in ((4, gain), (12, dv)):
+            nc.sync.dma_start(
+                out=vec_rows[row : row + 4, :].rearrange("t (q i) -> t q i", i=8),
+                in_=vec[512:1024].rearrange("(q t i) -> t q i", t=PACK, i=8),
+            )
+        nc.sync.dma_start(out=vec_rows[16:20, :], in_=fv.rearrange("(u p) -> u p", p=P))
+        load_w4(1)
+        wgs_dealt = held("wgs_dealt", [P, PACK, S], F32)
+        for q in range(16):
+            rows = wgs[32 * (q % 4) : 32 * (q % 4 + 1), :]
+            nc.sync.dma_start(out=wgs_dealt[8 * q : 8 * q + 8], in_=rows.rearrange("(t i) c -> i t c", i=8))
+        for u in (3, 4, 5):
+            load_page(u)
+        jv_all = held("jv_all", [P, NP], F32)
+        nc.sync.dma_start(out=jv_all[:], in_=jv.partition_broadcast(P))
+
+        v_scales = [held(f"v_scales{a}", [P, S], U8) for a in range(PASSES)]
+        v_words = [held(f"v_words{a}", [P, S], U32) for a in range(PASSES)]
+
+        stage_main = held("stage_main", [P, 2048], BF16)
+        stage_second = shared("stage_second", [P, 2048], BF16, "row_first", 1)
+        stage_fifth = held("stage_fifth", [P, 2048], BF16)
+        stage = [{1: stage_second, 4: stage_fifth}.get(u, stage_main)[:] for u in range(TILES)]
+        w_codes, gw, h = {}, {}, {0: stage_second[:, 0:1024].bitcast(F32)}
+        w_planes = [held(f"w_planes{n}", [P, 512], U8) for n in range(3)]
+        tanh_d = [held(f"tanh_d{n}", [P, S], F32)[:] for n in range(2)] * 4
+        tanh_b = [held(f"tanh_b{n}", [P, S], F32)[:] for n in range(2)] * 4
+        for u in (1, 2):
+            tanh_d[u] = raw[u + 1, 0, 0][:].rearrange("p j c -> p (j c)")
+            tanh_b[u] = raw[u + 1, 0, 1][:].rearrange("p j c -> p (j c)")
+        fetched = [held(f"fetched{n}", [P, NP], F32)[:] for n in range(3)] * 3
+
+        def row_tag(u):
+            return "row_first" if u < 0 else f"row{u}"
+
+        w4_dealt = held("w4_dealt", [P, PASSES, 1024], U8)
+        w4_planes_dealt = held("w4_planes_dealt", [P, PASSES, 512], U8)
+        woven = {(half, which): held(f"woven{half}{which}", [P, NP, PACK], BF16) for half in range(2) for which in range(2)}
+        moved = shared("moved", [P, PACK, 2, NP], BF16, "large", 2)
+        planes1 = held("planes1", [P, PACK, 2 * NP], BF16)
+        picked = [held(f"picked{u}", [P, 2 * NP], BF16)[:] for u in range(HALF - 1)]
+        picked = picked + [shared("picked3", [P, 2 * NP], BF16, "page6", 1)[:]] + [planes1[:, t, :] for t in range(PACK)]
+
+        def cast(u, copy):
+            for n in (2, 3, 0, 1):
+                w, a = divmod(n, 2)
+                dst = stage[u][:, 512 * n : 512 * (n + 1)]
+                if u < HALF:
+                    copy(
+                        out=dst.rearrange("p (c i j) -> p c j i", i=4, j=PACK),
+                        in_=raw[u, w, a][:].rearrange("p j (c i) -> p c j i", i=4),
+                    )
+                else:
+                    src = wide[w, a][:].rearrange("p j (q t h i) -> p t q h j i", t=PACK, h=2, i=4)
+                    copy(out=dst.rearrange("p (q h i j) -> p q h j i", h=2, i=4, j=PACK), in_=src[:, u - HALF])
+
+        def quantise_weights(u):
+            if u < 2:
+                w_codes[u] = held(f"w_codes{u}", [P, 512], U32)
+            else:
+                w_codes[u] = shared(f"w_codes{u}", [P, 512], U32, row_tag(u - 3), 1)
+            nc.vector.quantize_mx(out=w_codes[u][:].bitcast(FP8X4), scales=w_planes[u % 3][:], in_=stage[u])
+
+        def first_stage(u):
+            b_bank, d_bank = banks[2 * (u % 4)], banks[2 * (u % 4) + 1]
+            codes, planes = w_codes[u], w_planes[u % 3]
+
+            def product(bank, lhs, lhs_scale, a, start, stop):
+                nc.tensor.matmul_mx(
+                    out=bank[:], lhsT=lhs, lhsT_scale=lhs_scale, rhs=v_words[a][:].bitcast(FP8X4),
+                    rhs_scale=v_scales[a][:], start=start, stop=stop,
+                )
+
+            def fp8(n):
+                return codes[:, P * n : P * (n + 1)].bitcast(FP8X4), planes[:, P * n : P * (n + 1)]
+
+            def fp4(a):
+                words, scales = (w4_halves[0], w4_planes) if u < HALF else (w4_dealt, w4_planes_dealt)
+                c = u % HALF
+                return words[:, a, 256 * c : 256 * (c + 1)].bitcast(FP4X4), scales[:, a, P * c : P * (c + 1)]
+
+            product(d_bank, *fp8(2), 0, True, False)
+            product(b_bank, *fp8(0), 0, True, False)
+            product(b_bank, *fp4(0), 0, False, False)
+            product(d_bank, *fp8(3), 1, False, True)
+            product(b_bank, *fp8(1), 1, False, False)
+            product(b_bank, *fp4(1), 1, False, True)
+
+        def squash(u):
+            nc.scalar.activation(out=tanh_d[u], in_=banks[2 * (u % 4) + 1][:], func=ACT.Tanh)
+            nc.scalar.activation(out=tanh_b[u], in_=banks[2 * (u % 4)][:], func=ACT.Tanh)
+
+        def gained_factor(u):
+            factor = wgs_nat[:] if u < HALF else wgs_dealt[:, u - HALF, :]
+            gw[u] = shared(f"gw{u}", [P, S], F32, row_tag(u), 1)
+            nc.scalar.activation(out=gw[u][:], in_=factor, func=ACT.Copy, scale=(gain_first if u < HALF else vec_cols)[:, u : u + 1])
+
+        def larger(u):
+            if u > 0:
+                h[u] = shared(f"h{u}", [P, S], F32, row_tag(u - 1), 1)[:]
+            nc.vector.tensor_tensor(out=h[u], in0=tanh_b[u], in1=tanh_d[u], op=ALU.max)
+
+        def scatter(u):
+            nc.vector.tensor_tensor(
+                out=pages[u][:].indirect(idx2[:]), in0=h[u], in1=gw[u][:], op=ALU.mult
+            )
+
+        def finish_x2(u):
+            nc.scalar.activation(out=size[u], in_=fetched[u], func=ACT.Abs)
+            nc.scalar.activation(out=picked[u][:, NP:], in_=size[u], func=ACT.Copy, scale=vec_cols[:, 8 + u : 9 + u])
+            if u < HALF:
+                for t in range(PACK):
+                    nc.sync.dma_start(
+                        out=moved[32 * u : 32 * (u + 1), t].rearrange("p x c -> p (x c)"), in_=picked[u][t:P:PACK]
+                    )
+
+        moved_rows = [moved[:, t].rearrange("p x c -> p (x c)").bitcast(F32) for t in range(3)]
+        tanh_d[7], tanh_b[7] = moved_rows[0], moved_rows[1]
+        x_codes = {}
+        x_planes = {}
+
+        def weave(copy, half, which, planes, cols):
+            count = planes.shape[1]
+            copy(
+                out=woven[half, which][:, cols, 0:count].rearrange("p (c i) j -> p c j i", i=4),
+                in_=planes[:, :, cols].rearrange("p j (c i) -> p c j i", i=4),
+            )
+
+        def quantise_x(half, which, cols):
+            key = (half, which)
+            if key not in x_codes:
+                tag, bufs = (row_tag(5 + which), 1) if half == 0 else ("small", 12)
+                x_codes[key] = shared(f"x_codes{half}{which}", [P, NP], U32, tag, bufs)
+                x_planes[key] = held(f"x_planes{half}{which}", [P, NP], U8)
+            nc.vector.quantize_mx(
+                out=x_codes[key][:, cols].bitcast(FP8X4), scales=x_planes[key][:, cols],
+                in_=woven[key][:, cols, :].rearrange("p c j -> p (c j)"),
+            )
+
+        def second_stage(half, mt):
+            cols = slice(P * mt, P * (mt + 1))
+            nc.tensor.matmul_mx(
+                out=banks[mt][:], lhsT=x_codes[half, 0][:, cols].bitcast(FP8X4), lhsT_scale=x_planes[half, 0][:, cols],
+                rhs=x_codes[half, 1][:].bitcast(FP8X4), rhs_scale=x_planes[half, 1][:],
+                start=(half == 0), stop=(half == 1),
+            )
+
+        cast(0, nc.scalar.copy)
+        for a in range(PASSES):
+            nc.vector.tensor_copy(out=v_scales[a][:], in_=tab_planes[:, a, :].indirect(idx[:]))
+            nc.vector.tensor_copy(out=v_words[a][:], in_=tab[a][:].indirect(idx[:]))
+            if a == 0:
+                quantise_weights(0)
+        first_stage(0)
+        cast(1, nc.vector.tensor_copy)
+        quantise_weights(1)
+        first_stage(1)
+        for u in range(HALF):
+            gained_factor(u)
+        squash(0)
+        larger(0)
+        cast(2, nc.scalar.copy)
+        squash(1)
+        ident = shared("ident", [P, P], F32, "gate_b", 1)
+        make_identity(nc, ident[:])
+        nc.tensor.transpose(banks[0][:, 0:P], vec_rows[:], ident[:])
+        vec_cols = held("vec_cols", [P, 20], F32)
+        nc.scalar.copy(out=vec_cols[:], in_=banks[0][:, 0:20])
+        tanh_d[3] = shared("tanh_d3", [P, S], F32, "gate_d", 1)[:]
+        tanh_b[3] = shared("tanh_b3", [P, S], F32, "gate_b", 1)[:]
+        size = [tanh_b[3], tanh_d[3], tanh_d[4], tanh_b[4], tanh_d[5], moved_rows[2], tanh_d[6]]
+        nc.vector.tensor_copy(
+            out=w4_dealt[:].bitcast(I32).rearrange("p a (t q w) -> p a t q w", t=PACK, w=4),
+            in_=w4_halves[1][:].bitcast(I32).rearrange("p a (q t w) -> p a t q w", t=PACK, w=4),
+        )
+        nc.vector.tensor_copy(
+            out=w4_planes_dealt[:].bitcast(I32).rearrange("p a (t q w) -> p a t q w", t=PACK, w=2),
+            in_=w4_planes[:, :, 512:].bitcast(I32).rearrange("p a (q t w) -> p a t q w", t=PACK, w=2),
+        )
+        halves = (slice(0, 256), slice(256, 512))
+
+        for u in range(TILES):
+            scatter(u)
+            if u + 1 < TILES:
+                nc.vector.tensor_copy(out=fetched[u], in_=pages[u][:].indirect(idx4[:]))
+            if u + 2 < TILES:
+                quantise_weights(u + 2)
+                first_stage(u + 2)
+            else:
+                quantise_x(0, u + 2 - TILES, slice(0, NP))
+            if u + 1 == TILES:
+                continue
+            larger(u + 1)
+            nc.vector.tensor_copy(out=picked[u][:, 0:NP], in_=pages[u][:].indirect(idx3[:]))
+            if u + 3 < TILES:
+                cast(u + 3, nc.scalar.copy)
+            for v in {2: (0, 1), 3: (2, 3)}.get(u, (u,) if u >= HALF else ()):
+                finish_x2(v)
+            if u == HALF - 1:
+                load_page(6)
+                load_page(7)
+            if u + 2 < TILES:
+                squash(u + 2)
+            if u == 2:
+                for v in range(HALF, TILES):
+                    gained_factor(v)
+            if u == HALF:
+                for which in range(2):
+                    for cols in halves:
+                        weave(nc.scalar.copy, 0, which, moved[:, :, which, :], cols)
+
+        last = TILES - 1
+        for mt in range(4):
+            second_stage(0, mt)
+        last_x2 = shared("last_x2", [P, NP], F32, "small", 12)
+        last_size = shared("last_size", [P, NP], F32, "small", 12)
+        weave(nc.scalar.copy, 1, 1, planes1[:, 0:3, NP:], slice(0, NP))
+        for n, cols in enumerate(halves):
+            nc.vector.tensor_copy(out=last_x2[:, cols], in_=pages[last][:].indirect(idx4[:, 16 * n : 16 * (n + 1)]))
+            nc.scalar.activation(out=last_size[:, cols], in_=last_x2[:, cols], func=ACT.Abs)
+            nc.scalar.activation(
+                out=woven[1, 1][:, cols, 3], in_=last_size[:, cols], func=ACT.Copy, scale=vec_cols[:, 15:16]
+            )
+        for n, cols in enumerate(halves):
+            nc.vector.tensor_copy(out=picked[last][:, cols], in_=pages[last][:].indirect(idx3[:, 16 * n : 16 * (n + 1)]))
+        for cols in halves:
+            weave(nc.vector.tensor_copy, 1, 0, planes1[:, :, 0:NP], cols)
+        quantise_x(1, 0, halves[0])
+        quantise_x(1, 1, slice(0, NP))
+        quantise_x(1, 0, halves[1])
+        for mt in range(4):
+            second_stage(1, mt)
+        for mt in range(4):
+            result = shared(f"result{mt}", [P, NP], F32, "small", 12)
+            nc.vector.scalar_tensor_tensor(
+                out=result[:], in0=banks[mt][:], scalar=vec_cols[:, 16 + mt : 17 + mt], in1=jv_all[:],
+                op0=ALU.add, op1=ALU.mult,
+            )
+            nc.sync.dma_start(out=out[P * mt : P * (mt + 1), :], in_=result[:])

@@ -44,10 +44,14 @@ def tile_list_braze_wetting_scores_kernel(
 
         tab_planes = held("tab_planes", [P, PASSES, T], U8)
         w4_planes = held("w4_planes", [P, PASSES, H], U8)
-        vec_rows = shared("vec_rows", [P, P], F32, "gate_d", 1)
+        vec_rows = held("vec_rows", [P, P], F32)
+        fv_rows = shared("fv_rows", [P, P], F32, "fourth", 1)
+        vec_cols = held("vec_cols", [P, 2 * TILES], F32)
+        fv_cols = held("fv_cols", [P, 4], F32)
         nc.vector.memset(tab_planes[:].bitcast(I32), 0)
-        nc.vector.memset(vec_rows[:], 0.0)
         nc.vector.memset(w4_planes[:].bitcast(I32), 0)
+        nc.vector.memset(vec_rows[:], 0.0)
+        nc.vector.memset(fv_rows[:], 0.0)
 
         idx = lists.tile([P, S // 16], U16, name="idx")
         idx2 = lists.tile([P, S // 16], U16, name="idx2")
@@ -61,8 +65,11 @@ def tile_list_braze_wetting_scores_kernel(
                 for a in range(PASSES):
                     if u >= 2 and w == 0:
                         raw[u, w, a] = held(f"raw{u}{w}{a}", [P, PACK, P], F32)
+                    elif u >= 2 and (u, a) != (3, 1):
+                        tag = {(2, 0): "row3", (2, 1): "turned", (3, 0): "size_first"}[u, a]
+                        raw[u, w, a] = shared(f"raw{u}{w}{a}", [P, PACK, P], F32, tag, 1)
                     else:
-                        raw[u, w, a] = shared(f"raw{u}{w}{a}", [P, PACK, P], F32, "small", 12)
+                        raw[u, w, a] = shared(f"raw{u}{w}{a}", [P, PACK, P], F32, "small", 9)
                     rows = weights[w][512 * a : 512 * (a + 1), P * u : P * (u + 1)]
                     nc.sync.dma_start(out=raw[u, w, a][:], in_=rows.rearrange("(p j) c -> p j c", j=PACK))
 
@@ -89,10 +96,10 @@ def tile_list_braze_wetting_scores_kernel(
         def load_table(a):
             nc.sync.dma_start(out=tab[a][:].bitcast(I32), in_=tab_words[a].rearrange("p t i -> p (t i)").bitcast(I32))
 
-        load_natural_weights(0, (1,))
         load_table(0)
-        load_natural_weights(0, (0,))
+        load_natural_weights(0, (1,))
         load_scales(nc.sync, tab_planes, tab_scales)
+        load_natural_weights(0, (0,))
         load_table(1)
         w4_halves = [held(f"w4_half{n}", [P, PASSES, 1024], U8) for n in range(2)]
 
@@ -103,9 +110,16 @@ def tile_list_braze_wetting_scores_kernel(
         load_w4(0)
 
         load_scales(nc.gpsimd, w4_planes, w4_scales)
-        gain_first = held("gain_first", [P, HALF], F32)
-        with nc.allow_non_contiguous_dma(reason="one gain a partition"):
-            nc.sync.dma_start(out=gain_first[:], in_=gain[0:512].rearrange("(u p) -> p u", p=P))
+        for row, vec in ((0, gain), (8, dv)):
+            nc.sync.dma_start(out=vec_rows[row : row + 4, :], in_=vec[0:512].rearrange("(u p) -> u p", p=P))
+            nc.sync.dma_start(
+                out=vec_rows[row + 4 : row + 8, :].rearrange("t (q i) -> t q i", i=8),
+                in_=vec[512:].rearrange("(q t i) -> t q i", t=PACK, i=8),
+            )
+        ident = held("ident", [P, P], F32)
+        make_identity(nc, ident[:])
+        nc.tensor.transpose(banks[7][:, 0:P], vec_rows[:], ident[:])
+        nc.scalar.copy(out=vec_cols[:], in_=banks[7][:, 0:16])
         wgs_nat = held("wgs_nat", [P, S], F32)
         nc.sync.dma_start(out=wgs_nat[:], in_=wgs)
         load_natural_weights(1)
@@ -114,8 +128,8 @@ def tile_list_braze_wetting_scores_kernel(
         nc.sync.dma_start(idx4[:], offs4)
         nc.sync.dma_start(idx3[:], offs3)
         load_natural_weights(2)
-        load_page(1)
         load_natural_weights(3)
+        load_page(1)
         wide = {}
 
         def load_wide(w, a):
@@ -128,19 +142,9 @@ def tile_list_braze_wetting_scores_kernel(
         load_page(2)
         load_wide(0, 0)
         load_wide(0, 1)
-        nc.sync.dma_start(out=vec_rows[8:12, :], in_=dv[0:512].rearrange("(u p) -> u p", p=P))
-        for row, vec in ((4, gain), (12, dv)):
-            nc.sync.dma_start(
-                out=vec_rows[row : row + 4, :].rearrange("t (q i) -> t q i", i=8),
-                in_=vec[512:1024].rearrange("(q t i) -> t q i", t=PACK, i=8),
-            )
-        nc.sync.dma_start(out=vec_rows[16:20, :], in_=fv.rearrange("(u p) -> u p", p=P))
+        nc.sync.dma_start(out=fv_rows[0:4, :], in_=fv.rearrange("(u p) -> u p", p=P))
         load_w4(1)
-        wgs_dealt = held("wgs_dealt", [P, PACK, S], F32)
-        for q in range(16):
-            rows = wgs[32 * (q % 4) : 32 * (q % 4 + 1), :]
-            nc.sync.dma_start(out=wgs_dealt[8 * q : 8 * q + 8], in_=rows.rearrange("(t i) c -> i t c", i=8))
-        for u in (3, 4, 5):
+        for u in range(3, TILES):
             load_page(u)
         jv_all = held("jv_all", [P, NP], F32)
         nc.sync.dma_start(out=jv_all[:], in_=jv.partition_broadcast(P))
@@ -151,26 +155,30 @@ def tile_list_braze_wetting_scores_kernel(
         stage_main = held("stage_main", [P, 2048], BF16)
         stage_second = shared("stage_second", [P, 2048], BF16, "row_first", 1)
         stage_fifth = held("stage_fifth", [P, 2048], BF16)
-        stage = [{1: stage_second, 4: stage_fifth}.get(u, stage_main)[:] for u in range(TILES)]
+        stage = [stage_main[:], stage_second[:], stage_main[:], stage_main[:]] + [stage_fifth[:]] * HALF
         w_codes, gw, h = {}, {}, {0: stage_second[:, 0:1024].bitcast(F32)}
         w_planes = [held(f"w_planes{n}", [P, 512], U8) for n in range(3)]
-        tanh_d = [held(f"tanh_d{n}", [P, S], F32)[:] for n in range(2)] * 4
+        tanh_d = [None] * TILES
         tanh_b = [held(f"tanh_b{n}", [P, S], F32)[:] for n in range(2)] * 4
         for u in (1, 2):
             tanh_d[u] = raw[u + 1, 0, 0][:].rearrange("p j c -> p (j c)")
             tanh_b[u] = raw[u + 1, 0, 1][:].rearrange("p j c -> p (j c)")
-        fetched = [held(f"fetched{n}", [P, NP], F32)[:] for n in range(3)] * 3
+        fetched = [held(f"fetched{n}", [P, NP], F32)[:] for n in range(3)]
+        fetched = fetched + [fetched[2]] * 4
+        tanh_d[0] = shared("tanh_d_first", [P, S], F32, "row1", 1)[:]
+        tanh_b[0] = shared("tanh_b_first", [P, S], F32, "row2", 1)[:]
 
         def row_tag(u):
             return "row_first" if u < 0 else f"row{u}"
 
         w4_dealt = held("w4_dealt", [P, PASSES, 1024], U8)
-        w4_planes_dealt = held("w4_planes_dealt", [P, PASSES, 512], U8)
         woven = {(half, which): held(f"woven{half}{which}", [P, NP, PACK], BF16) for half in range(2) for which in range(2)}
         moved = shared("moved", [P, PACK, 2, NP], BF16, "large", 2)
-        planes1 = held("planes1", [P, PACK, 2 * NP], BF16)
+        planes1 = held("planes1", [P, PACK * 2 * NP], BF16)
         picked = [held(f"picked{u}", [P, 2 * NP], BF16)[:] for u in range(HALF - 1)]
-        picked = picked + [shared("picked3", [P, 2 * NP], BF16, "page6", 1)[:]] + [planes1[:, t, :] for t in range(PACK)]
+        picked = picked + [None] + [planes1[:, 2 * NP * t : 2 * NP * (t + 1)] for t in range(PACK)]
+        for u in range(HALF, TILES - 1):
+            tanh_d[u] = picked[u].bitcast(F32)
 
         def cast(u, copy):
             for n in (2, 3, 0, 1):
@@ -189,11 +197,11 @@ def tile_list_braze_wetting_scores_kernel(
             if u < 2:
                 w_codes[u] = held(f"w_codes{u}", [P, 512], U32)
             else:
-                w_codes[u] = shared(f"w_codes{u}", [P, 512], U32, row_tag(u - 3), 1)
+                w_codes[u] = shared(f"w_codes{u}", [P, 512], U32, "row_first" if u == 2 else f"page{u - 3}", 1)
             nc.vector.quantize_mx(out=w_codes[u][:].bitcast(FP8X4), scales=w_planes[u % 3][:], in_=stage[u])
 
         def first_stage(u):
-            b_bank, d_bank = banks[2 * (u % 4)], banks[2 * (u % 4) + 1]
+            b_bank, d_bank = banks[2 * (u % 2)], banks[2 * (u % 2) + 1]
             codes, planes = w_codes[u], w_planes[u % 3]
 
             def product(bank, lhs, lhs_scale, a, start, stop):
@@ -218,13 +226,36 @@ def tile_list_braze_wetting_scores_kernel(
             product(b_bank, *fp4(1), 1, False, True)
 
         def squash(u):
-            nc.scalar.activation(out=tanh_d[u], in_=banks[2 * (u % 4) + 1][:], func=ACT.Tanh)
-            nc.scalar.activation(out=tanh_b[u], in_=banks[2 * (u % 4)][:], func=ACT.Tanh)
+            nc.scalar.activation(out=tanh_d[u], in_=banks[2 * (u % 2) + 1][:], func=ACT.Tanh)
+            nc.scalar.activation(out=tanh_b[u], in_=banks[2 * (u % 2)][:], func=ACT.Tanh)
 
         def gained_factor(u):
-            factor = wgs_nat[:] if u < HALF else wgs_dealt[:, u - HALF, :]
+            factor = wgs_nat[:] if u < HALF else banks[5][:]
             gw[u] = shared(f"gw{u}", [P, S], F32, row_tag(u), 1)
-            nc.scalar.activation(out=gw[u][:], in_=factor, func=ACT.Copy, scale=(gain_first if u < HALF else vec_cols)[:, u : u + 1])
+            nc.scalar.activation(out=gw[u][:], in_=factor, func=ACT.Copy, scale=vec_cols[:, u : u + 1])
+
+
+        def turn_wgs():
+            for jb in range(4):
+                nc.tensor.transpose(banks[4][:, P * jb : P * (jb + 1)], wgs_nat[:, P * jb : P * (jb + 1)], ident[:])
+            for t in range(PACK):
+                src = banks[4][:].rearrange("p (b q t i) -> p t b q i", b=4, t=PACK, i=8)[:, t]
+                nc.scalar.copy(
+                    out=turned[:, t].rearrange("p b (g q i) -> p b g q i", g=4, i=8),
+                    in_=src.unsqueeze(2).to_broadcast([P, 4, 4, 4, 8]),
+                )
+
+        def turn_back(t):
+            for jb in range(4):
+                nc.tensor.transpose(banks[5][:, P * jb : P * (jb + 1)], turned[:, t, jb, :], ident[:])
+
+        def turn_fv():
+            nc.tensor.transpose(banks[5][:, 0:P], fv_rows[:], ident[:])
+            nc.scalar.copy(out=fv_cols[:], in_=banks[5][:, 0:4])
+            fourth = shared("fourth", [P, 4 * NP], BF16, "fourth", 1)
+            picked[3] = fourth[:, 0 : 2 * NP]
+            tanh_d[3] = picked[3].bitcast(F32)
+            tanh_b[3] = fourth[:, 2 * NP :].bitcast(F32)
 
         def larger(u):
             if u > 0:
@@ -236,9 +267,11 @@ def tile_list_braze_wetting_scores_kernel(
                 out=pages[u][:].indirect(idx2[:]), in0=h[u], in1=gw[u][:], op=ALU.mult
             )
 
-        def finish_x2(u):
+        def magnitude(u):
             nc.scalar.activation(out=size[u], in_=fetched[u], func=ACT.Abs)
-            nc.scalar.activation(out=picked[u][:, NP:], in_=size[u], func=ACT.Copy, scale=vec_cols[:, 8 + u : 9 + u])
+
+        def finish_x2(u):
+            nc.scalar.activation(out=picked[u][:, NP:], in_=size[u], func=ACT.Copy, scale=vec_cols[:, TILES + u : TILES + u + 1])
             if u < HALF:
                 for t in range(PACK):
                     nc.sync.dma_start(
@@ -250,28 +283,28 @@ def tile_list_braze_wetting_scores_kernel(
         x_codes = {}
         x_planes = {}
 
-        def weave(copy, half, which, planes, cols):
+        def weave(copy, dst, planes, cols):
             count = planes.shape[1]
             copy(
-                out=woven[half, which][:, cols, 0:count].rearrange("p (c i) j -> p c j i", i=4),
+                out=dst[:, cols, 0:count].rearrange("p (c i) j -> p c j i", i=4),
                 in_=planes[:, :, cols].rearrange("p j (c i) -> p c j i", i=4),
             )
 
-        def quantise_x(half, which, cols):
+        def quantise_x(half, which, cols, src):
             key = (half, which)
             if key not in x_codes:
-                tag, bufs = (row_tag(5 + which), 1) if half == 0 else ("small", 12)
+                tag, bufs = (f"page{5 + which}", 1) if half == 0 else ("small", 9)
                 x_codes[key] = shared(f"x_codes{half}{which}", [P, NP], U32, tag, bufs)
                 x_planes[key] = held(f"x_planes{half}{which}", [P, NP], U8)
             nc.vector.quantize_mx(
                 out=x_codes[key][:, cols].bitcast(FP8X4), scales=x_planes[key][:, cols],
-                in_=woven[key][:, cols, :].rearrange("p c j -> p (c j)"),
+                in_=src[:, cols, :].rearrange("p c j -> p (c j)"),
             )
 
         def second_stage(half, mt):
             cols = slice(P * mt, P * (mt + 1))
             nc.tensor.matmul_mx(
-                out=banks[mt][:], lhsT=x_codes[half, 0][:, cols].bitcast(FP8X4), lhsT_scale=x_planes[half, 0][:, cols],
+                out=banks[4 + mt][:], lhsT=x_codes[half, 0][:, cols].bitcast(FP8X4), lhsT_scale=x_planes[half, 0][:, cols],
                 rhs=x_codes[half, 1][:].bitcast(FP8X4), rhs_scale=x_planes[half, 1][:],
                 start=(half == 0), stop=(half == 1),
             )
@@ -286,85 +319,90 @@ def tile_list_braze_wetting_scores_kernel(
         cast(1, nc.vector.tensor_copy)
         quantise_weights(1)
         first_stage(1)
-        for u in range(HALF):
-            gained_factor(u)
+        gained_factor(0)
         squash(0)
         larger(0)
         cast(2, nc.scalar.copy)
+        turned = shared("wgs_turned", [P, PACK, 4, P], F32, "turned", 1)
+        for u in range(1, HALF):
+            gained_factor(u)
         squash(1)
-        ident = shared("ident", [P, P], F32, "gate_b", 1)
-        make_identity(nc, ident[:])
-        nc.tensor.transpose(banks[0][:, 0:P], vec_rows[:], ident[:])
-        vec_cols = held("vec_cols", [P, 20], F32)
-        nc.scalar.copy(out=vec_cols[:], in_=banks[0][:, 0:20])
-        tanh_d[3] = shared("tanh_d3", [P, S], F32, "gate_d", 1)[:]
-        tanh_b[3] = shared("tanh_b3", [P, S], F32, "gate_b", 1)[:]
-        size = [tanh_b[3], tanh_d[3], tanh_d[4], tanh_b[4], tanh_d[5], moved_rows[2], tanh_d[6]]
         nc.vector.tensor_copy(
             out=w4_dealt[:].bitcast(I32).rearrange("p a (t q w) -> p a t q w", t=PACK, w=4),
             in_=w4_halves[1][:].bitcast(I32).rearrange("p a (q t w) -> p a t q w", t=PACK, w=4),
-        )
-        nc.vector.tensor_copy(
-            out=w4_planes_dealt[:].bitcast(I32).rearrange("p a (t q w) -> p a t q w", t=PACK, w=2),
-            in_=w4_planes[:, :, 512:].bitcast(I32).rearrange("p a (q t w) -> p a t q w", t=PACK, w=2),
         )
         halves = (slice(0, 256), slice(256, 512))
 
         for u in range(TILES):
             scatter(u)
-            if u + 1 < TILES:
-                nc.vector.tensor_copy(out=fetched[u], in_=pages[u][:].indirect(idx4[:]))
             if u + 2 < TILES:
                 quantise_weights(u + 2)
                 first_stage(u + 2)
             else:
-                quantise_x(0, u + 2 - TILES, slice(0, NP))
+                quantise_x(0, u + 2 - TILES, slice(0, NP), woven[0, u + 2 - TILES])
             if u + 1 == TILES:
                 continue
+            nc.vector.tensor_copy(out=fetched[u], in_=pages[u][:].indirect(idx4[:]))
             larger(u + 1)
             nc.vector.tensor_copy(out=picked[u][:, 0:NP], in_=pages[u][:].indirect(idx3[:]))
             if u + 3 < TILES:
                 cast(u + 3, nc.scalar.copy)
-            for v in {2: (0, 1), 3: (2, 3)}.get(u, (u,) if u >= HALF else ()):
-                finish_x2(v)
-            if u == HALF - 1:
-                load_page(6)
-                load_page(7)
-            if u + 2 < TILES:
-                squash(u + 2)
-            if u == 2:
-                for v in range(HALF, TILES):
-                    gained_factor(v)
-            if u == HALF:
+            if u == 5:
                 for which in range(2):
                     for cols in halves:
-                        weave(nc.scalar.copy, 0, which, moved[:, :, which, :], cols)
+                        weave(nc.scalar.copy, woven[0, which], moved[:, :, which, :], cols)
+            if u >= 2:
+                magnitude(u)
+            if u + 2 < TILES:
+                squash(u + 2)
+            if u >= 2:
+                finish_x2(u)
+            if u == 0:
+                turn_wgs()
+                turn_fv()
+                size_first = shared("size_first", [P, NP], F32, "size_first", 1)[:]
+                size = [size_first, size_first] + tanh_d[3:6] + [moved_rows[2], picked[7].bitcast(F32)]
+            if u == 1:
+                w4_planes_dealt = shared("w4_planes_dealt", [P, PASSES, 512], U8, "row0", 1)
+                nc.vector.tensor_copy(
+                    out=w4_planes_dealt[:].bitcast(I32).rearrange("p a (t q w) -> p a t q w", t=PACK, w=2),
+                    in_=w4_planes[:, :, 512:].bitcast(I32).rearrange("p a (q t w) -> p a t q w", t=PACK, w=2),
+                )
+            if 2 <= u < 6:
+                gained_factor(u + 2)
+            if 1 <= u < 5:
+                turn_back(u - 1)
+            if u == 1:
+                for v in range(2):
+                    magnitude(v)
+                    finish_x2(v)
 
         last = TILES - 1
+        planes_last = planes1[:].rearrange("p (t x) -> p t x", t=PACK)
         for mt in range(4):
             second_stage(0, mt)
-        last_x2 = shared("last_x2", [P, NP], F32, "small", 12)
-        last_size = shared("last_size", [P, NP], F32, "small", 12)
-        weave(nc.scalar.copy, 1, 1, planes1[:, 0:3, NP:], slice(0, NP))
+        last_x2 = shared("last_x2", [P, NP], F32, "small", 9)
+        weave(nc.scalar.copy, woven[1, 1], planes_last[:, 0:3, NP:], slice(0, NP))
         for n, cols in enumerate(halves):
             nc.vector.tensor_copy(out=last_x2[:, cols], in_=pages[last][:].indirect(idx4[:, 16 * n : 16 * (n + 1)]))
-            nc.scalar.activation(out=last_size[:, cols], in_=last_x2[:, cols], func=ACT.Abs)
+            last_size = picked[HALF + n][:, NP:].bitcast(F32)
+            nc.scalar.activation(out=last_size, in_=last_x2[:, cols], func=ACT.Abs)
             nc.scalar.activation(
-                out=woven[1, 1][:, cols, 3], in_=last_size[:, cols], func=ACT.Copy, scale=vec_cols[:, 15:16]
+                out=woven[1, 1][:, cols, 3], in_=last_size, func=ACT.Copy, scale=vec_cols[:, TILES + last : TILES + last + 1]
             )
         for n, cols in enumerate(halves):
             nc.vector.tensor_copy(out=picked[last][:, cols], in_=pages[last][:].indirect(idx3[:, 16 * n : 16 * (n + 1)]))
-        for cols in halves:
-            weave(nc.vector.tensor_copy, 1, 0, planes1[:, :, 0:NP], cols)
-        quantise_x(1, 0, halves[0])
-        quantise_x(1, 1, slice(0, NP))
-        quantise_x(1, 0, halves[1])
+        weave(nc.vector.tensor_copy, woven[1, 0], planes_last[:, :, 0:NP], halves[0])
+        quantise_x(1, 1, slice(0, NP), woven[1, 1])
+        quantise_x(1, 0, halves[0], woven[1, 0])
+        weave(nc.vector.tensor_copy, woven[1, 1], planes_last[:, :, 0:NP], halves[1])
+        quantise_x(1, 0, halves[1], woven[1, 1])
         for mt in range(4):
             second_stage(1, mt)
         for mt in range(4):
-            result = shared(f"result{mt}", [P, NP], F32, "small", 12)
+            result = shared(f"result{mt}", [P, NP], F32, "small", 9)
             nc.vector.scalar_tensor_tensor(
-                out=result[:], in0=banks[mt][:], scalar=vec_cols[:, 16 + mt : 17 + mt], in1=jv_all[:],
+                out=result[:], in0=banks[4 + mt][:], scalar=fv_cols[:, mt : mt + 1], in1=jv_all[:],
                 op0=ALU.add, op1=ALU.mult,
             )
             nc.sync.dma_start(out=out[P * mt : P * (mt + 1), :], in_=result[:])

@@ -44,11 +44,13 @@ def tile_list_braze_wetting_scores_kernel(
 
         tab_planes = held("tab_planes", [P, PASSES, T], U8)
         w4_planes = held("w4_planes", [P, PASSES, H], U8)
+        gain_rows = held("gain_rows", [P, P], F32)
         vec_rows = held("vec_rows", [P, P], F32)
         fv_rows = shared("fv_rows", [P, P], F32, "fourth", 1)
         vec_cols = held("vec_cols", [P, 2 * TILES], F32)
         fv_cols = held("fv_cols", [P, 4], F32)
         nc.vector.memset(tab_planes[:].bitcast(I32), 0)
+        nc.vector.memset(gain_rows[:], 0.0)
         nc.vector.memset(w4_planes[:].bitcast(I32), 0)
         nc.vector.memset(vec_rows[:], 0.0)
         nc.vector.memset(fv_rows[:], 0.0)
@@ -63,13 +65,8 @@ def tile_list_braze_wetting_scores_kernel(
         def load_natural_weights(u, which=(1, 0)):
             for w in which:
                 for a in range(PASSES):
-                    if u >= 2 and w == 0:
-                        raw[u, w, a] = held(f"raw{u}{w}{a}", [P, PACK, P], F32)
-                    elif u >= 2 and (u, a) != (3, 1):
-                        tag = {(2, 0): "row3", (2, 1): "turned", (3, 0): "size_first"}[u, a]
-                        raw[u, w, a] = shared(f"raw{u}{w}{a}", [P, PACK, P], F32, tag, 1)
-                    else:
-                        raw[u, w, a] = shared(f"raw{u}{w}{a}", [P, PACK, P], F32, "small", 9)
+                    tag, bufs = (f"raw{u}{w}{a}", 1) if u >= 2 or (w, a) == (0, 1) else ("small", 6)
+                    raw[u, w, a] = shared(f"raw{u}{w}{a}", [P, PACK, P], F32, tag, bufs)
                     rows = weights[w][512 * a : 512 * (a + 1), P * u : P * (u + 1)]
                     nc.sync.dma_start(out=raw[u, w, a][:], in_=rows.rearrange("(p j) c -> p j c", j=PACK))
 
@@ -96,9 +93,9 @@ def tile_list_braze_wetting_scores_kernel(
         def load_table(a):
             nc.sync.dma_start(out=tab[a][:].bitcast(I32), in_=tab_words[a].rearrange("p t i -> p (t i)").bitcast(I32))
 
-        load_table(0)
         load_natural_weights(0, (1,))
         load_scales(nc.sync, tab_planes, tab_scales)
+        load_table(0)
         load_natural_weights(0, (0,))
         load_table(1)
         w4_halves = [held(f"w4_half{n}", [P, PASSES, 1024], U8) for n in range(2)]
@@ -109,25 +106,27 @@ def tile_list_braze_wetting_scores_kernel(
 
         load_w4(0)
 
-        load_scales(nc.gpsimd, w4_planes, w4_scales)
-        for row, vec in ((0, gain), (8, dv)):
-            nc.sync.dma_start(out=vec_rows[row : row + 4, :], in_=vec[0:512].rearrange("(u p) -> u p", p=P))
-            nc.sync.dma_start(
-                out=vec_rows[row + 4 : row + 8, :].rearrange("t (q i) -> t q i", i=8),
-                in_=vec[512:].rearrange("(q t i) -> t q i", t=PACK, i=8),
-            )
         ident = held("ident", [P, P], F32)
         make_identity(nc, ident[:])
-        nc.tensor.transpose(banks[7][:, 0:P], vec_rows[:], ident[:])
-        nc.scalar.copy(out=vec_cols[:], in_=banks[7][:, 0:16])
+        nc.gpsimd.dma_start(out=gain_rows[0:4, :], in_=gain[0:512].rearrange("(u p) -> u p", p=P))
+        load_scales(nc.sync, w4_planes, w4_scales)
+        nc.tensor.transpose(banks[6][:, 0:P], gain_rows[:], ident[:])
+        gain_first = shared("gain_first", [P, HALF], F32, "raw001", 1)
+        nc.scalar.copy(out=gain_first[:], in_=banks[6][:, 0:HALF])
+        load_natural_weights(1)
         wgs_nat = held("wgs_nat", [P, S], F32)
         nc.sync.dma_start(out=wgs_nat[:], in_=wgs)
-        load_natural_weights(1)
         load_page(0)
         nc.sync.dma_start(idx2[:], offs2)
         nc.sync.dma_start(idx4[:], offs4)
         nc.sync.dma_start(idx3[:], offs3)
         load_natural_weights(2)
+        nc.sync.dma_start(out=vec_rows[8:12, :], in_=dv[0:512].rearrange("(u p) -> u p", p=P))
+        for row, vec in ((4, gain), (12, dv)):
+            nc.sync.dma_start(
+                out=vec_rows[row : row + 4, :].rearrange("t (q i) -> t q i", i=8),
+                in_=vec[512:].rearrange("(q t i) -> t q i", t=PACK, i=8),
+            )
         load_natural_weights(3)
         load_page(1)
         wide = {}
@@ -153,30 +152,27 @@ def tile_list_braze_wetting_scores_kernel(
         v_words = [held(f"v_words{a}", [P, S], U32) for a in range(PASSES)]
 
         stage_main = held("stage_main", [P, 2048], BF16)
-        stage_second = shared("stage_second", [P, 2048], BF16, "row_first", 1)
+        stage_second = held("stage_second", [P, 2048], BF16)
         stage_fifth = held("stage_fifth", [P, 2048], BF16)
         stage = [stage_main[:], stage_second[:], stage_main[:], stage_main[:]] + [stage_fifth[:]] * HALF
-        w_codes, gw, h = {}, {}, {0: stage_second[:, 0:1024].bitcast(F32)}
+        w_codes, gw, h = {}, {}, {}
         w_planes = [held(f"w_planes{n}", [P, 512], U8) for n in range(3)]
         tanh_d = [None] * TILES
         tanh_b = [held(f"tanh_b{n}", [P, S], F32)[:] for n in range(2)] * 4
-        for u in (1, 2):
-            tanh_d[u] = raw[u + 1, 0, 0][:].rearrange("p j c -> p (j c)")
-            tanh_b[u] = raw[u + 1, 0, 1][:].rearrange("p j c -> p (j c)")
-        fetched = [held(f"fetched{n}", [P, NP], F32)[:] for n in range(3)]
-        fetched = fetched + [fetched[2]] * 4
+        spent = {key: tile[:].rearrange("p j c -> p (j c)") for key, tile in raw.items()}
+        tanh_d[1], tanh_b[1], fetched = spent[2, 0, 0], spent[2, 1, 1], spent[2, 0, 1]
+        tanh_d[2], tanh_b[2] = spent[3, 0, 0], spent[3, 0, 1]
         tanh_d[0] = shared("tanh_d_first", [P, S], F32, "row1", 1)[:]
-        tanh_b[0] = shared("tanh_b_first", [P, S], F32, "row2", 1)[:]
+        tanh_b[0] = tanh_b[4]
 
         def row_tag(u):
-            return "row_first" if u < 0 else f"row{u}"
+            return {-1: "raw101", 2: "raw200", 3: "raw211", 5: "page1", 7: "page3"}.get(u, f"row{u}")
 
         w4_dealt = held("w4_dealt", [P, PASSES, 1024], U8)
-        woven = {(half, which): held(f"woven{half}{which}", [P, NP, PACK], BF16) for half in range(2) for which in range(2)}
+        woven = {(half, which): shared(f"woven{half}{which}", [P, NP, PACK], BF16, f"woven{half}{which}", 1) for half in range(2) for which in range(2)}
         moved = shared("moved", [P, PACK, 2, NP], BF16, "large", 2)
         planes1 = held("planes1", [P, PACK * 2 * NP], BF16)
-        picked = [held(f"picked{u}", [P, 2 * NP], BF16)[:] for u in range(HALF - 1)]
-        picked = picked + [None] + [planes1[:, 2 * NP * t : 2 * NP * (t + 1)] for t in range(PACK)]
+        picked = [spent[3, 1, a].bitcast(BF16) for a in range(PASSES)] + [None, None] + [planes1[:, 2 * NP * t : 2 * NP * (t + 1)] for t in range(PACK)]
         for u in range(HALF, TILES - 1):
             tanh_d[u] = picked[u].bitcast(F32)
 
@@ -194,10 +190,10 @@ def tile_list_braze_wetting_scores_kernel(
                     copy(out=dst.rearrange("p (q h i j) -> p q h j i", h=2, i=4, j=PACK), in_=src[:, u - HALF])
 
         def quantise_weights(u):
-            if u < 2:
+            if u < 3:
                 w_codes[u] = held(f"w_codes{u}", [P, 512], U32)
             else:
-                w_codes[u] = shared(f"w_codes{u}", [P, 512], U32, "row_first" if u == 2 else f"page{u - 3}", 1)
+                w_codes[u] = shared(f"w_codes{u}", [P, 512], U32, f"page{u - 3}", 1)
             nc.vector.quantize_mx(out=w_codes[u][:].bitcast(FP8X4), scales=w_planes[u % 3][:], in_=stage[u])
 
         def first_stage(u):
@@ -230,9 +226,9 @@ def tile_list_braze_wetting_scores_kernel(
             nc.scalar.activation(out=tanh_b[u], in_=banks[2 * (u % 2)][:], func=ACT.Tanh)
 
         def gained_factor(u):
-            factor = wgs_nat[:] if u < HALF else banks[5][:]
+            factor = wgs_nat[:] if u < HALF else banks[5 + u % 2][:]
             gw[u] = shared(f"gw{u}", [P, S], F32, row_tag(u), 1)
-            nc.scalar.activation(out=gw[u][:], in_=factor, func=ACT.Copy, scale=vec_cols[:, u : u + 1])
+            nc.scalar.activation(out=gw[u][:], in_=factor, func=ACT.Copy, scale=(gain_first if u < HALF else vec_cols)[:, u : u + 1])
 
 
         def turn_wgs():
@@ -247,19 +243,19 @@ def tile_list_braze_wetting_scores_kernel(
 
         def turn_back(t):
             for jb in range(4):
-                nc.tensor.transpose(banks[5][:, P * jb : P * (jb + 1)], turned[:, t, jb, :], ident[:])
+                nc.tensor.transpose(banks[5 + t % 2][:, P * jb : P * (jb + 1)], turned[:, t, jb, :], ident[:])
 
         def turn_fv():
             nc.tensor.transpose(banks[5][:, 0:P], fv_rows[:], ident[:])
             nc.scalar.copy(out=fv_cols[:], in_=banks[5][:, 0:4])
-            fourth = shared("fourth", [P, 4 * NP], BF16, "fourth", 1)
+            fourth = shared("fourth", [P, 6 * NP], BF16, "fourth", 1)
             picked[3] = fourth[:, 0 : 2 * NP]
             tanh_d[3] = picked[3].bitcast(F32)
-            tanh_b[3] = fourth[:, 2 * NP :].bitcast(F32)
+            tanh_b[3] = fourth[:, 2 * NP : 4 * NP].bitcast(F32)
+            picked[2] = fourth[:, 4 * NP :]
 
         def larger(u):
-            if u > 0:
-                h[u] = shared(f"h{u}", [P, S], F32, row_tag(u - 1), 1)[:]
+            h[u] = shared(f"h{u}", [P, S], F32, row_tag(u - 1), 1)[:]
             nc.vector.tensor_tensor(out=h[u], in0=tanh_b[u], in1=tanh_d[u], op=ALU.max)
 
         def scatter(u):
@@ -267,11 +263,14 @@ def tile_list_braze_wetting_scores_kernel(
                 out=pages[u][:].indirect(idx2[:]), in0=h[u], in1=gw[u][:], op=ALU.mult
             )
 
+        def size(u):
+            return moved_rows[2] if u == 5 else picked[u + 1].bitcast(F32)
+
         def magnitude(u):
-            nc.scalar.activation(out=size[u], in_=fetched[u], func=ACT.Abs)
+            nc.scalar.activation(out=size(u), in_=fetched, func=ACT.Abs)
 
         def finish_x2(u):
-            nc.scalar.activation(out=picked[u][:, NP:], in_=size[u], func=ACT.Copy, scale=vec_cols[:, TILES + u : TILES + u + 1])
+            nc.scalar.activation(out=picked[u][:, NP:], in_=size(u), func=ACT.Copy, scale=vec_cols[:, TILES + u : TILES + u + 1])
             if u < HALF:
                 for t in range(PACK):
                     nc.sync.dma_start(
@@ -293,7 +292,7 @@ def tile_list_braze_wetting_scores_kernel(
         def quantise_x(half, which, cols, src):
             key = (half, which)
             if key not in x_codes:
-                tag, bufs = (f"page{5 + which}", 1) if half == 0 else ("small", 9)
+                tag, bufs = (("page5", "row6")[which], 1) if half == 0 else ("small", 6)
                 x_codes[key] = shared(f"x_codes{half}{which}", [P, NP], U32, tag, bufs)
                 x_planes[key] = held(f"x_planes{half}{which}", [P, NP], U8)
             nc.vector.quantize_mx(
@@ -323,10 +322,11 @@ def tile_list_braze_wetting_scores_kernel(
         squash(0)
         larger(0)
         cast(2, nc.scalar.copy)
-        turned = shared("wgs_turned", [P, PACK, 4, P], F32, "turned", 1)
-        for u in range(1, HALF):
-            gained_factor(u)
+        turned = shared("wgs_turned", [P, PACK, 4, P], F32, "raw210", 1)
+        gained_factor(1)
         squash(1)
+        nc.tensor.transpose(banks[7][:, 0:P], vec_rows[:], ident[:])
+        nc.scalar.copy(out=vec_cols[:], in_=banks[7][:, 0:16])
         nc.vector.tensor_copy(
             out=w4_dealt[:].bitcast(I32).rearrange("p a (t q w) -> p a t q w", t=PACK, w=4),
             in_=w4_halves[1][:].bitcast(I32).rearrange("p a (q t w) -> p a t q w", t=PACK, w=4),
@@ -338,30 +338,29 @@ def tile_list_braze_wetting_scores_kernel(
             if u + 2 < TILES:
                 quantise_weights(u + 2)
                 first_stage(u + 2)
-            else:
-                quantise_x(0, u + 2 - TILES, slice(0, NP), woven[0, u + 2 - TILES])
+            elif u + 1 < TILES:
+                quantise_x(0, 0, slice(0, NP), woven[0, 0])
             if u + 1 == TILES:
                 continue
-            nc.vector.tensor_copy(out=fetched[u], in_=pages[u][:].indirect(idx4[:]))
+            nc.vector.tensor_copy(out=fetched, in_=pages[u][:].indirect(idx4[:]))
             larger(u + 1)
-            nc.vector.tensor_copy(out=picked[u][:, 0:NP], in_=pages[u][:].indirect(idx3[:]))
             if u + 3 < TILES:
                 cast(u + 3, nc.scalar.copy)
+            nc.vector.tensor_copy(out=picked[u][:, 0:NP], in_=pages[u][:].indirect(idx3[:]))
             if u == 5:
                 for which in range(2):
                     for cols in halves:
                         weave(nc.scalar.copy, woven[0, which], moved[:, :, which, :], cols)
-            if u >= 2:
-                magnitude(u)
+            if u == 1:
+                turn_fv()
+            magnitude(u)
             if u + 2 < TILES:
                 squash(u + 2)
-            if u >= 2:
-                finish_x2(u)
+            finish_x2(u)
             if u == 0:
+                gained_factor(2)
+                gained_factor(3)
                 turn_wgs()
-                turn_fv()
-                size_first = shared("size_first", [P, NP], F32, "size_first", 1)[:]
-                size = [size_first, size_first] + tanh_d[3:6] + [moved_rows[2], picked[7].bitcast(F32)]
             if u == 1:
                 w4_planes_dealt = shared("w4_planes_dealt", [P, PASSES, 512], U8, "row0", 1)
                 nc.vector.tensor_copy(
@@ -370,18 +369,15 @@ def tile_list_braze_wetting_scores_kernel(
                 )
             if 2 <= u < 6:
                 gained_factor(u + 2)
-            if 1 <= u < 5:
-                turn_back(u - 1)
             if u == 1:
-                for v in range(2):
-                    magnitude(v)
-                    finish_x2(v)
+                turn_back(0)
+                turn_back(1)
+            if 2 <= u < 4:
+                turn_back(u)
 
         last = TILES - 1
         planes_last = planes1[:].rearrange("p (t x) -> p t x", t=PACK)
-        for mt in range(4):
-            second_stage(0, mt)
-        last_x2 = shared("last_x2", [P, NP], F32, "small", 9)
+        last_x2 = shared("last_x2", [P, NP], F32, "small", 6)
         weave(nc.scalar.copy, woven[1, 1], planes_last[:, 0:3, NP:], slice(0, NP))
         for n, cols in enumerate(halves):
             nc.vector.tensor_copy(out=last_x2[:, cols], in_=pages[last][:].indirect(idx4[:, 16 * n : 16 * (n + 1)]))
@@ -390,17 +386,20 @@ def tile_list_braze_wetting_scores_kernel(
             nc.scalar.activation(
                 out=woven[1, 1][:, cols, 3], in_=last_size, func=ACT.Copy, scale=vec_cols[:, TILES + last : TILES + last + 1]
             )
+        quantise_x(0, 1, slice(0, NP), woven[0, 1])
+        for mt in range(4):
+            second_stage(0, mt)
         for n, cols in enumerate(halves):
             nc.vector.tensor_copy(out=picked[last][:, cols], in_=pages[last][:].indirect(idx3[:, 16 * n : 16 * (n + 1)]))
         weave(nc.vector.tensor_copy, woven[1, 0], planes_last[:, :, 0:NP], halves[0])
         quantise_x(1, 1, slice(0, NP), woven[1, 1])
         quantise_x(1, 0, halves[0], woven[1, 0])
-        weave(nc.vector.tensor_copy, woven[1, 1], planes_last[:, :, 0:NP], halves[1])
-        quantise_x(1, 0, halves[1], woven[1, 1])
+        weave(nc.scalar.copy, woven[1, 0], planes_last[:, :, 0:NP], halves[1])
+        quantise_x(1, 0, halves[1], woven[1, 0])
         for mt in range(4):
             second_stage(1, mt)
         for mt in range(4):
-            result = shared(f"result{mt}", [P, NP], F32, "small", 9)
+            result = shared(f"result{mt}", [P, NP], F32, *(("woven10", 1) if mt == 0 else ("small", 6)))
             nc.vector.scalar_tensor_tensor(
                 out=result[:], in0=banks[4 + mt][:], scalar=fv_cols[:, mt : mt + 1], in1=jv_all[:],
                 op0=ALU.add, op1=ALU.mult,

@@ -43,15 +43,17 @@ def tile_list_braze_wetting_scores_kernel(
         weights = (w1, w3)
 
         tab_planes = held("tab_planes", [P, PASSES, T], U8)
-        w4_planes = held("w4_planes", [P, PASSES, H], U8)
+        w4_planes = [held(f"w4_planes{n}", [P, PASSES, 512], U8) for n in range(2)]
         gain_rows = held("gain_rows", [P, P], F32)
         vec_rows = held("vec_rows", [P, P], F32)
         fv_rows = shared("fv_rows", [P, P], F32, "fourth", 1)
         vec_cols = held("vec_cols", [P, 2 * TILES], F32)
         fv_cols = held("fv_cols", [P, 4], F32)
-        nc.vector.memset(tab_planes[:].bitcast(I32), 0)
+        nc.vector.memset(tab_planes[:, 0, :].bitcast(I32), 0)
+        nc.gpsimd.memset(tab_planes[:, 1, :].bitcast(I32), 0)
         nc.vector.memset(gain_rows[:], 0.0)
-        nc.vector.memset(w4_planes[:].bitcast(I32), 0)
+        for planes in w4_planes:
+            nc.vector.memset(planes[:].bitcast(I32), 0)
         nc.vector.memset(vec_rows[:], 0.0)
         nc.vector.memset(fv_rows[:], 0.0)
 
@@ -80,9 +82,9 @@ def tile_list_braze_wetting_scores_kernel(
                 rows = page0[512:, :].rearrange("(q t i) c -> t q i c", t=PACK, i=8)
                 nc.sync.dma_start(out=pages[u][:], in_=rows[u - HALF])
 
-        def load_scales(queue, planes, src):
+        def load_scales(planes, src):
             for quad in range(4):
-                queue.dma_start(
+                nc.sync.dma_start(
                     out=planes[32 * quad : 32 * quad + 4].bitcast(I32),
                     in_=src[:, 4 * quad : 4 * quad + 4, :].rearrange("a r c -> r a c").bitcast(I32),
                 )
@@ -93,29 +95,29 @@ def tile_list_braze_wetting_scores_kernel(
         def load_table(a):
             nc.sync.dma_start(out=tab[a][:].bitcast(I32), in_=tab_words[a].rearrange("p t i -> p (t i)").bitcast(I32))
 
-        load_natural_weights(0, (1,))
-        load_scales(nc.sync, tab_planes, tab_scales)
-        load_table(0)
-        load_natural_weights(0, (0,))
-        load_table(1)
         w4_halves = [held(f"w4_half{n}", [P, PASSES, 1024], U8) for n in range(2)]
 
         def load_w4(n):
             src = w4_words[:, :, 1024 * n : 1024 * (n + 1)].rearrange("a p c -> p a c")
             nc.sync.dma_start(out=w4_halves[n][:].bitcast(I32), in_=src.bitcast(I32))
 
-        load_w4(0)
-
         ident = held("ident", [P, P], F32)
         make_identity(nc, ident[:])
-        nc.gpsimd.dma_start(out=gain_rows[0:4, :], in_=gain[0:512].rearrange("(u p) -> u p", p=P))
-        load_scales(nc.sync, w4_planes, w4_scales)
+        wgs_nat = held("wgs_nat", [P, S], F32)
+        load_natural_weights(0, (1,))
+        load_scales(tab_planes, tab_scales)
+        load_table(0)
+        nc.sync.dma_start(out=gain_rows[0:4, :], in_=gain[0:512].rearrange("(u p) -> u p", p=P))
+        load_natural_weights(0, (0,))
+        load_table(1)
+        load_w4(0)
+        load_scales(w4_planes[0], w4_scales[:, :, 0:512])
+        load_natural_weights(1, (1,))
+        load_natural_weights(1, (0,))
+        nc.sync.dma_start(out=wgs_nat[:], in_=wgs)
         nc.tensor.transpose(banks[6][:, 0:P], gain_rows[:], ident[:])
         gain_first = shared("gain_first", [P, HALF], F32, "raw001", 1)
         nc.scalar.copy(out=gain_first[:], in_=banks[6][:, 0:HALF])
-        load_natural_weights(1)
-        wgs_nat = held("wgs_nat", [P, S], F32)
-        nc.sync.dma_start(out=wgs_nat[:], in_=wgs)
         load_page(0)
         nc.sync.dma_start(idx2[:], offs2)
         nc.sync.dma_start(idx4[:], offs4)
@@ -129,6 +131,7 @@ def tile_list_braze_wetting_scores_kernel(
             )
         load_natural_weights(3)
         load_page(1)
+        load_scales(w4_planes[1], w4_scales[:, :, 512:])
         wide = {}
 
         def load_wide(w, a):
@@ -160,19 +163,20 @@ def tile_list_braze_wetting_scores_kernel(
         tanh_d = [None] * TILES
         tanh_b = [held(f"tanh_b{n}", [P, S], F32)[:] for n in range(2)] * 4
         spent = {key: tile[:].rearrange("p j c -> p (j c)") for key, tile in raw.items()}
-        tanh_d[1], tanh_b[1], fetched = spent[2, 0, 0], spent[2, 1, 1], spent[2, 0, 1]
+        tanh_d[1], tanh_b[1] = spent[2, 0, 0], spent[2, 0, 1]
+        fetched = held("fetched", [P, NP], F32)[:]
         tanh_d[2], tanh_b[2] = spent[3, 0, 0], spent[3, 0, 1]
         tanh_d[0] = shared("tanh_d_first", [P, S], F32, "row1", 1)[:]
         tanh_b[0] = tanh_b[4]
 
         def row_tag(u):
-            return {-1: "raw101", 2: "raw200", 3: "raw211", 5: "page1", 7: "page3"}.get(u, f"row{u}")
+            return {-1: "raw101", 2: "raw200", 3: "raw201", 5: "page1", 7: "page3"}.get(u, f"row{u}")
 
         w4_dealt = held("w4_dealt", [P, PASSES, 1024], U8)
         woven = {(half, which): shared(f"woven{half}{which}", [P, NP, PACK], BF16, f"woven{half}{which}", 1) for half in range(2) for which in range(2)}
         moved = shared("moved", [P, PACK, 2, NP], BF16, "large", 2)
         planes1 = held("planes1", [P, PACK * 2 * NP], BF16)
-        picked = [spent[3, 1, a].bitcast(BF16) for a in range(PASSES)] + [None, None] + [planes1[:, 2 * NP * t : 2 * NP * (t + 1)] for t in range(PACK)]
+        picked = [held("picked0", [P, 2 * NP], BF16)[:], spent[3, 1, 1].bitcast(BF16)] + [tanh_d[2].bitcast(BF16), None] + [planes1[:, 2 * NP * t : 2 * NP * (t + 1)] for t in range(PACK)]
         for u in range(HALF, TILES - 1):
             tanh_d[u] = picked[u].bitcast(F32)
 
@@ -210,7 +214,7 @@ def tile_list_braze_wetting_scores_kernel(
                 return codes[:, P * n : P * (n + 1)].bitcast(FP8X4), planes[:, P * n : P * (n + 1)]
 
             def fp4(a):
-                words, scales = (w4_halves[0], w4_planes) if u < HALF else (w4_dealt, w4_planes_dealt)
+                words, scales = (w4_halves[0], w4_planes[0]) if u < HALF else (w4_dealt, w4_planes_dealt)
                 c = u % HALF
                 return words[:, a, 256 * c : 256 * (c + 1)].bitcast(FP4X4), scales[:, a, P * c : P * (c + 1)]
 
@@ -248,11 +252,10 @@ def tile_list_braze_wetting_scores_kernel(
         def turn_fv():
             nc.tensor.transpose(banks[5][:, 0:P], fv_rows[:], ident[:])
             nc.scalar.copy(out=fv_cols[:], in_=banks[5][:, 0:4])
-            fourth = shared("fourth", [P, 6 * NP], BF16, "fourth", 1)
+            fourth = shared("fourth", [P, 4 * NP], BF16, "fourth", 1)
             picked[3] = fourth[:, 0 : 2 * NP]
             tanh_d[3] = picked[3].bitcast(F32)
             tanh_b[3] = fourth[:, 2 * NP : 4 * NP].bitcast(F32)
-            picked[2] = fourth[:, 4 * NP :]
 
         def larger(u):
             h[u] = shared(f"h{u}", [P, S], F32, row_tag(u - 1), 1)[:]
@@ -325,8 +328,8 @@ def tile_list_braze_wetting_scores_kernel(
         turned = shared("wgs_turned", [P, PACK, 4, P], F32, "raw210", 1)
         gained_factor(1)
         squash(1)
-        nc.tensor.transpose(banks[7][:, 0:P], vec_rows[:], ident[:])
-        nc.scalar.copy(out=vec_cols[:], in_=banks[7][:, 0:16])
+        nc.tensor.transpose(banks[4][:, 0:P], vec_rows[:], ident[:])
+        nc.scalar.copy(out=vec_cols[:], in_=banks[4][:, 0:16])
         nc.vector.tensor_copy(
             out=w4_dealt[:].bitcast(I32).rearrange("p a (t q w) -> p a t q w", t=PACK, w=4),
             in_=w4_halves[1][:].bitcast(I32).rearrange("p a (q t w) -> p a t q w", t=PACK, w=4),
@@ -365,7 +368,7 @@ def tile_list_braze_wetting_scores_kernel(
                 w4_planes_dealt = shared("w4_planes_dealt", [P, PASSES, 512], U8, "row0", 1)
                 nc.vector.tensor_copy(
                     out=w4_planes_dealt[:].bitcast(I32).rearrange("p a (t q w) -> p a t q w", t=PACK, w=2),
-                    in_=w4_planes[:, :, 512:].bitcast(I32).rearrange("p a (q t w) -> p a t q w", t=PACK, w=2),
+                    in_=w4_planes[1][:].bitcast(I32).rearrange("p a (q t w) -> p a t q w", t=PACK, w=2),
                 )
             if 2 <= u < 6:
                 gained_factor(u + 2)

@@ -19,9 +19,26 @@ ACT = mybir.ActivationFunctionType
 
 P = 128
 PACK = 4
-PASSES = 2
-TILES = 8
-HALF = 4
+SPAN = P * PACK
+PASSES = K // SPAN
+GROUP = 8
+QUADS = 4
+QUAD_SIZE = P // QUADS
+SCALE_ROWS = QUAD_SIZE // GROUP
+TILES = H // P
+HALF = TILES // 2
+LAST = TILES - 1
+OUT_TILES = NP // P
+LINE = 4
+W1, W3 = 0, 1
+PIECES = ((W3, 0), (W3, 1), (W1, 0), (W1, 1))
+X1, X2 = 0, 1
+SMALL_BUFS = 6
+PLANE_RING = 3
+CODES_LAG = 3
+BANK_COLS = 512
+E_BANK = 4
+TURN_BANK, BACK_BANK, GAIN_BANK = 4, 5, 6
 
 
 def tile_list_braze_wetting_scores_kernel(
@@ -36,19 +53,22 @@ def tile_list_braze_wetting_scores_kernel(
         def held(name, shape, dtype):
             return keep.tile(shape, dtype, name=name, align_bytes=64)
 
-        def shared(name, shape, dtype, tag, bufs):
+        def shared(name, shape, dtype, tag, bufs=1):
             return keep.tile(shape, dtype, name=name, tag=tag, bufs=bufs, align_bytes=64)
 
-        banks = [psum.tile([P, 512], F32, name=f"bank{n}") for n in range(8)]
-        weights = (w1, w3)
+        def piece_tag(u, w, a):
+            return f"raw{u}{w}{a}"
+
+        banks = [psum.tile([P, BANK_COLS], F32, name=f"bank{n}") for n in range(8)]
+        weights = {W1: w1, W3: w3}
 
         tab_planes = held("tab_planes", [P, PASSES, T], U8)
-        w4_planes = [held(f"w4_planes{n}", [P, PASSES, 512], U8) for n in range(2)]
+        w4_planes = [held(f"w4_planes{n}", [P, PASSES, H // 2], U8) for n in range(2)]
         gain_rows = held("gain_rows", [P, P], F32)
         vec_rows = held("vec_rows", [P, P], F32)
-        fv_rows = shared("fv_rows", [P, P], F32, "fourth", 1)
-        vec_cols = held("vec_cols", [P, 2 * TILES], F32)
-        fv_cols = held("fv_cols", [P, 4], F32)
+        fv_rows = shared("fv_rows", [P, P], F32, "tile3")
+        vec_cols = held("vec_cols", [P, HALF + TILES], F32)
+        fv_cols = held("fv_cols", [P, OUT_TILES], F32)
         nc.vector.memset(tab_planes[:, 0, :].bitcast(I32), 0)
         nc.gpsimd.memset(tab_planes[:, 1, :].bitcast(I32), 0)
         nc.vector.memset(gain_rows[:], 0.0)
@@ -62,89 +82,84 @@ def tile_list_braze_wetting_scores_kernel(
         idx3 = lists.tile([P, NP // 16], U16, name="idx3")
         idx4 = lists.tile([P, NP // 16], U16, name="idx4")
 
-        raw = {}
+        raw, wide, pages = {}, {}, {}
 
-        def load_natural_weights(u, which=(1, 0)):
-            for w in which:
-                for a in range(PASSES):
-                    tag, bufs = (f"raw{u}{w}{a}", 1) if u >= 2 or (w, a) == (0, 1) else ("small", 6)
-                    raw[u, w, a] = shared(f"raw{u}{w}{a}", [P, PACK, P], F32, tag, bufs)
-                    rows = weights[w][512 * a : 512 * (a + 1), P * u : P * (u + 1)]
-                    nc.sync.dma_start(out=raw[u, w, a][:], in_=rows.rearrange("(p j) c -> p j c", j=PACK))
+        def load_natural_weights(u, pieces=PIECES):
+            for w, a in pieces:
+                handed_on = u >= 2 or (w, a) == PIECES[-1]
+                tag, bufs = (piece_tag(u, w, a), 1) if handed_on else ("small", SMALL_BUFS)
+                raw[u, w, a] = shared(f"raw{u}{w}{a}", [P, PACK, P], F32, tag, bufs)
+                rows = weights[w][SPAN * a : SPAN * (a + 1), P * u : P * (u + 1)]
+                nc.sync.dma_start(out=raw[u, w, a][:], in_=rows.rearrange("(p j) c -> p j c", j=PACK))
 
-        pages = {}
+        def load_wide(w, a):
+            wide[w, a] = held(f"wide{w}{a}", [P, PACK, H // 2], F32)
+            rows = weights[w][SPAN * a : SPAN * (a + 1), H // 2 :]
+            nc.sync.dma_start(out=wide[w, a][:], in_=rows.rearrange("(p j) c -> p j c", j=PACK))
 
         def load_page(u):
-            pages[u] = shared(f"page{u}", [P, T2], F32, f"page{u}", 1)
+            pages[u] = shared(f"page{u}", [P, T2], F32, f"page{u}")
             if u < HALF:
                 nc.sync.dma_start(out=pages[u][:], in_=page0[P * u : P * (u + 1), :])
             else:
-                rows = page0[512:, :].rearrange("(q t i) c -> t q i c", t=PACK, i=8)
+                rows = page0[H // 2 :, :].rearrange("(q t i) c -> t q i c", t=PACK, i=GROUP)
                 nc.sync.dma_start(out=pages[u][:], in_=rows[u - HALF])
 
         def load_scales(planes, src):
-            for quad in range(4):
+            for quad in range(QUADS):
                 nc.sync.dma_start(
-                    out=planes[32 * quad : 32 * quad + 4].bitcast(I32),
-                    in_=src[:, 4 * quad : 4 * quad + 4, :].rearrange("a r c -> r a c").bitcast(I32),
+                    out=planes[QUAD_SIZE * quad : QUAD_SIZE * quad + SCALE_ROWS].bitcast(I32),
+                    in_=src[:, SCALE_ROWS * quad : SCALE_ROWS * (quad + 1), :].rearrange("a r c -> r a c").bitcast(I32),
                 )
 
         nc.sync.dma_start(idx[:], offs)
-        tab = [shared(f"tab{a}", [P, T], U32, "large", 2) for a in range(PASSES)]
+        tab = [shared(f"tab{a}", [P, T], U32, "large", PASSES) for a in range(PASSES)]
 
         def load_table(a):
             nc.sync.dma_start(out=tab[a][:].bitcast(I32), in_=tab_words[a].rearrange("p t i -> p (t i)").bitcast(I32))
 
-        w4_halves = [held(f"w4_half{n}", [P, PASSES, 1024], U8) for n in range(2)]
+        w4_halves = [held(f"w4_half{n}", [P, PASSES, H], U8) for n in range(2)]
 
         def load_w4(n):
-            src = w4_words[:, :, 1024 * n : 1024 * (n + 1)].rearrange("a p c -> p a c")
+            src = w4_words[:, :, H * n : H * (n + 1)].rearrange("a p c -> p a c")
             nc.sync.dma_start(out=w4_halves[n][:].bitcast(I32), in_=src.bitcast(I32))
 
         ident = held("ident", [P, P], F32)
         make_identity(nc, ident[:])
         wgs_nat = held("wgs_nat", [P, S], F32)
-        load_natural_weights(0, (1,))
+        load_natural_weights(0, PIECES[:2])
         load_scales(tab_planes, tab_scales)
         load_table(0)
-        nc.sync.dma_start(out=gain_rows[0:4, :], in_=gain[0:512].rearrange("(u p) -> u p", p=P))
-        load_natural_weights(0, (0,))
+        nc.sync.dma_start(out=gain_rows[0:HALF, :], in_=gain[0 : H // 2].rearrange("(u p) -> u p", p=P))
+        load_natural_weights(0, PIECES[2:])
         load_table(1)
         load_w4(0)
-        load_scales(w4_planes[0], w4_scales[:, :, 0:512])
-        load_natural_weights(1, (1,))
-        load_natural_weights(1, (0,))
+        load_scales(w4_planes[0], w4_scales[:, :, 0 : H // 2])
+        load_natural_weights(1)
         nc.sync.dma_start(out=wgs_nat[:], in_=wgs)
-        nc.tensor.transpose(banks[6][:, 0:P], gain_rows[:], ident[:])
-        gain_first = shared("gain_first", [P, HALF], F32, "raw001", 1)
-        nc.scalar.copy(out=gain_first[:], in_=banks[6][:, 0:HALF])
+        nc.tensor.transpose(banks[GAIN_BANK][:, 0:P], gain_rows[:], ident[:])
+        gain_first = shared("gain_first", [P, HALF], F32, piece_tag(0, *PIECES[-1]))
+        nc.scalar.copy(out=gain_first[:], in_=banks[GAIN_BANK][:, 0:HALF])
         load_page(0)
         nc.sync.dma_start(idx2[:], offs2)
         nc.sync.dma_start(idx4[:], offs4)
         nc.sync.dma_start(idx3[:], offs3)
         load_natural_weights(2)
-        nc.sync.dma_start(out=vec_rows[8:12, :], in_=dv[0:512].rearrange("(u p) -> u p", p=P))
-        for row, vec in ((4, gain), (12, dv)):
+        nc.sync.dma_start(out=vec_rows[HALF:TILES, :], in_=dv[0 : H // 2].rearrange("(u p) -> u p", p=P))
+        for row, vec in ((0, gain), (TILES, dv)):
             nc.sync.dma_start(
-                out=vec_rows[row : row + 4, :].rearrange("t (q i) -> t q i", i=8),
-                in_=vec[512:].rearrange("(q t i) -> t q i", t=PACK, i=8),
+                out=vec_rows[row : row + HALF, :].rearrange("t (q i) -> t q i", i=GROUP),
+                in_=vec[H // 2 :].rearrange("(q t i) -> t q i", t=PACK, i=GROUP),
             )
-        load_natural_weights(3)
+        load_natural_weights(3, PIECES[:1])
         load_page(1)
-        load_scales(w4_planes[1], w4_scales[:, :, 512:])
-        wide = {}
-
-        def load_wide(w, a):
-            wide[w, a] = held(f"wide{w}{a}", [P, PACK, 512], F32)
-            rows = weights[w][512 * a : 512 * (a + 1), 512:]
-            nc.sync.dma_start(out=wide[w, a][:], in_=rows.rearrange("(p j) c -> p j c", j=PACK))
-
-        load_wide(1, 0)
-        load_wide(1, 1)
-        load_page(2)
-        load_wide(0, 0)
-        load_wide(0, 1)
-        nc.sync.dma_start(out=fv_rows[0:4, :], in_=fv.rearrange("(u p) -> u p", p=P))
+        load_natural_weights(3, PIECES[1:])
+        load_scales(w4_planes[1], w4_scales[:, :, H // 2 :])
+        for n, (w, a) in enumerate(PIECES):
+            load_wide(w, a)
+            if n == 1:
+                load_page(2)
+        nc.sync.dma_start(out=fv_rows[0:OUT_TILES, :], in_=fv.rearrange("(u p) -> u p", p=P))
         load_w4(1)
         for u in range(3, TILES):
             load_page(u)
@@ -154,162 +169,187 @@ def tile_list_braze_wetting_scores_kernel(
         v_scales = [held(f"v_scales{a}", [P, S], U8) for a in range(PASSES)]
         v_words = [held(f"v_words{a}", [P, S], U32) for a in range(PASSES)]
 
-        stage_main = held("stage_main", [P, 2048], BF16)
-        stage_second = held("stage_second", [P, 2048], BF16)
-        stage_fifth = held("stage_fifth", [P, 2048], BF16)
-        stage = [stage_main[:], stage_second[:], stage_main[:], stage_main[:]] + [stage_fifth[:]] * HALF
+        stage_main = shared("stage_main", [P, len(PIECES) * SPAN], BF16, "stage_main")
+        stage_second = held("stage_second", [P, len(PIECES) * SPAN], BF16)
+        stage_dealt = held("stage_dealt", [P, len(PIECES) * SPAN], BF16)
+        stage = [stage_main[:], stage_second[:], stage_main[:], stage_main[:]] + [stage_dealt[:]] * HALF
         w_codes, gw, h = {}, {}, {}
-        w_planes = [held(f"w_planes{n}", [P, 512], U8) for n in range(3)]
+        w_planes = [held(f"w_planes{n}", [P, len(PIECES) * P], U8) for n in range(PLANE_RING)]
         tanh_d = [None] * TILES
-        tanh_b = [held(f"tanh_b{n}", [P, S], F32)[:] for n in range(2)] * 4
-        spent = {key: tile[:].rearrange("p j c -> p (j c)") for key, tile in raw.items()}
-        tanh_d[1], tanh_b[1] = spent[2, 0, 0], spent[2, 0, 1]
-        fetched = held("fetched", [P, NP], F32)[:]
-        tanh_d[2], tanh_b[2] = spent[3, 0, 0], spent[3, 0, 1]
-        tanh_d[0] = shared("tanh_d_first", [P, S], F32, "row1", 1)[:]
-        tanh_b[0] = tanh_b[4]
+        tanh_b = [held(f"tanh_b{n}", [P, S], F32)[:] for n in range(2)] * HALF
+        after = {u: shared(f"after{u}", [P, 3 * S], F32, piece_tag(u, *PIECES[-1])) for u in (2, 3)}
+        for u in (1, 2):
+            tanh_d[u], tanh_b[u] = after[u + 1][:, 0:S], after[u + 1][:, S : 2 * S]
+        fetched = after[2][:, 2 * S :]
+        tanh_d[0] = shared("tanh_d_first", [P, S], F32, "row1")[:]
 
         def row_tag(u):
-            return {-1: "raw101", 2: "raw200", 3: "raw201", 5: "page1", 7: "page3"}.get(u, f"row{u}")
+            taken_over = {
+                -1: piece_tag(1, *PIECES[-1]),
+                2: piece_tag(3, *PIECES[1]),
+                3: piece_tag(3, *PIECES[2]),
+                5: f"page{4 - CODES_LAG}",
+                7: f"page{6 - CODES_LAG}",
+            }
+            return taken_over.get(u, f"row{u}")
 
-        w4_dealt = held("w4_dealt", [P, PASSES, 1024], U8)
-        woven = {(half, which): shared(f"woven{half}{which}", [P, NP, PACK], BF16, f"woven{half}{which}", 1) for half in range(2) for which in range(2)}
-        moved = shared("moved", [P, PACK, 2, NP], BF16, "large", 2)
-        planes1 = held("planes1", [P, PACK * 2 * NP], BF16)
-        picked = [held("picked0", [P, 2 * NP], BF16)[:], spent[3, 1, 1].bitcast(BF16)] + [tanh_d[2].bitcast(BF16), None] + [planes1[:, 2 * NP * t : 2 * NP * (t + 1)] for t in range(PACK)]
-        for u in range(HALF, TILES - 1):
+        w4_dealt = held("w4_dealt", [P, PASSES, H], U8)
+        woven = {
+            (half, which): held(f"woven{half}{which}", [P, NP // 2 if (half, which) == (1, X1) else NP, PACK], BF16)
+            for half in range(2)
+            for which in (X1, X2)
+        }
+        moved = shared("moved", [P, PACK, 2, NP], BF16, "large", PASSES)
+        dealt_x = shared("dealt_x", [P, PACK * 2 * NP], BF16, "dealt_x")
+        picked = [
+            raw[3, W3, 0][:].rearrange("p j c -> p (j c)").bitcast(BF16),
+            after[3][:, 2 * S :].bitcast(BF16),
+            tanh_d[2].bitcast(BF16),
+            None,
+        ] + [dealt_x[:, 2 * NP * t : 2 * NP * (t + 1)] for t in range(PACK)]
+        for u in range(HALF, LAST):
             tanh_d[u] = picked[u].bitcast(F32)
+        moved_rows = [moved[:, t].rearrange("p x c -> p (x c)").bitcast(F32) for t in range(3)]
+        tanh_d[LAST], tanh_b[LAST], size_after_weave = moved_rows
 
         def cast(u, copy):
-            for n in (2, 3, 0, 1):
-                w, a = divmod(n, 2)
-                dst = stage[u][:, 512 * n : 512 * (n + 1)]
+            for w, a in PIECES:
+                n = PASSES * w + a
+                dst = stage[u][:, SPAN * n : SPAN * (n + 1)]
                 if u < HALF:
                     copy(
-                        out=dst.rearrange("p (c i j) -> p c j i", i=4, j=PACK),
-                        in_=raw[u, w, a][:].rearrange("p j (c i) -> p c j i", i=4),
+                        out=dst.rearrange("p (c i j) -> p c j i", i=LINE, j=PACK),
+                        in_=raw[u, w, a][:].rearrange("p j (c i) -> p c j i", i=LINE),
                     )
                 else:
-                    src = wide[w, a][:].rearrange("p j (q t h i) -> p t q h j i", t=PACK, h=2, i=4)
-                    copy(out=dst.rearrange("p (q h i j) -> p q h j i", h=2, i=4, j=PACK), in_=src[:, u - HALF])
+                    src = wide[w, a][:].rearrange("p j (q t g i) -> p t q g j i", t=PACK, g=GROUP // LINE, i=LINE)
+                    copy(
+                        out=dst.rearrange("p (q g i j) -> p q g j i", g=GROUP // LINE, i=LINE, j=PACK),
+                        in_=src[:, u - HALF],
+                    )
 
         def quantise_weights(u):
-            if u < 3:
-                w_codes[u] = held(f"w_codes{u}", [P, 512], U32)
+            if u < CODES_LAG:
+                w_codes[u] = held(f"w_codes{u}", [P, len(PIECES) * P], U32)
             else:
-                w_codes[u] = shared(f"w_codes{u}", [P, 512], U32, f"page{u - 3}", 1)
-            nc.vector.quantize_mx(out=w_codes[u][:].bitcast(FP8X4), scales=w_planes[u % 3][:], in_=stage[u])
+                w_codes[u] = shared(f"w_codes{u}", [P, len(PIECES) * P], U32, f"page{u - CODES_LAG}")
+            nc.vector.quantize_mx(out=w_codes[u][:].bitcast(FP8X4), scales=w_planes[u % PLANE_RING][:], in_=stage[u])
+
+        def b_bank(u):
+            return banks[2 * (u % 2)]
+
+        def d_bank(u):
+            return banks[2 * (u % 2) + 1]
 
         def first_stage(u):
-            b_bank, d_bank = banks[2 * (u % 2)], banks[2 * (u % 2) + 1]
-            codes, planes = w_codes[u], w_planes[u % 3]
-
             def product(bank, lhs, lhs_scale, a, start, stop):
                 nc.tensor.matmul_mx(
                     out=bank[:], lhsT=lhs, lhsT_scale=lhs_scale, rhs=v_words[a][:].bitcast(FP8X4),
                     rhs_scale=v_scales[a][:], start=start, stop=stop,
                 )
 
-            def fp8(n):
-                return codes[:, P * n : P * (n + 1)].bitcast(FP8X4), planes[:, P * n : P * (n + 1)]
+            def fp8(w, a):
+                cols = slice(P * (PASSES * w + a), P * (PASSES * w + a + 1))
+                return w_codes[u][:, cols].bitcast(FP8X4), w_planes[u % PLANE_RING][:, cols]
 
             def fp4(a):
                 words, scales = (w4_halves[0], w4_planes[0]) if u < HALF else (w4_dealt, w4_planes_dealt)
                 c = u % HALF
-                return words[:, a, 256 * c : 256 * (c + 1)].bitcast(FP4X4), scales[:, a, P * c : P * (c + 1)]
+                return words[:, a, 2 * P * c : 2 * P * (c + 1)].bitcast(FP4X4), scales[:, a, P * c : P * (c + 1)]
 
-            product(d_bank, *fp8(2), 0, True, False)
-            product(b_bank, *fp8(0), 0, True, False)
-            product(b_bank, *fp4(0), 0, False, False)
-            product(d_bank, *fp8(3), 1, False, True)
-            product(b_bank, *fp8(1), 1, False, False)
-            product(b_bank, *fp4(1), 1, False, True)
+            for a in range(PASSES):
+                first, final = a == 0, a == PASSES - 1
+                product(d_bank(u), *fp8(W3, a), a, first, final)
+                product(b_bank(u), *fp8(W1, a), a, first, False)
+                product(b_bank(u), *fp4(a), a, False, final)
 
         def squash(u):
-            nc.scalar.activation(out=tanh_d[u], in_=banks[2 * (u % 2) + 1][:], func=ACT.Tanh)
-            nc.scalar.activation(out=tanh_b[u], in_=banks[2 * (u % 2)][:], func=ACT.Tanh)
+            nc.scalar.activation(out=tanh_d[u], in_=d_bank(u)[:], func=ACT.Tanh)
+            nc.scalar.activation(out=tanh_b[u], in_=b_bank(u)[:], func=ACT.Tanh)
+
+        def larger(u):
+            h[u] = shared(f"h{u}", [P, S], F32, row_tag(u - 1))[:]
+            nc.vector.tensor_tensor(out=h[u], in0=tanh_b[u], in1=tanh_d[u], op=ALU.max)
 
         def gained_factor(u):
-            factor = wgs_nat[:] if u < HALF else banks[5 + u % 2][:]
-            gw[u] = shared(f"gw{u}", [P, S], F32, row_tag(u), 1)
-            nc.scalar.activation(out=gw[u][:], in_=factor, func=ACT.Copy, scale=(gain_first if u < HALF else vec_cols)[:, u : u + 1])
-
+            if u < HALF:
+                factor, gains = wgs_nat[:], gain_first[:, u : u + 1]
+            else:
+                factor, gains = banks[BACK_BANK + u % 2][:], vec_cols[:, u - HALF : u - HALF + 1]
+            gw[u] = shared(f"gw{u}", [P, S], F32, row_tag(u))
+            nc.scalar.activation(out=gw[u][:], in_=factor, func=ACT.Copy, scale=gains)
 
         def turn_wgs():
-            for jb in range(4):
-                nc.tensor.transpose(banks[4][:, P * jb : P * (jb + 1)], wgs_nat[:, P * jb : P * (jb + 1)], ident[:])
+            for jb in range(S // P):
+                cols = slice(P * jb, P * (jb + 1))
+                nc.tensor.transpose(banks[TURN_BANK][:, cols], wgs_nat[:, cols], ident[:])
             for t in range(PACK):
-                src = banks[4][:].rearrange("p (b q t i) -> p t b q i", b=4, t=PACK, i=8)[:, t]
+                src = banks[TURN_BANK][:].rearrange("p (b q t i) -> p t b q i", b=S // P, t=PACK, i=GROUP)[:, t]
                 nc.scalar.copy(
-                    out=turned[:, t].rearrange("p b (g q i) -> p b g q i", g=4, i=8),
-                    in_=src.unsqueeze(2).to_broadcast([P, 4, 4, 4, 8]),
+                    out=turned[:, t].rearrange("p b (g q i) -> p b g q i", g=QUADS, i=GROUP),
+                    in_=src.unsqueeze(2).to_broadcast([P, S // P, QUADS, P // (PACK * GROUP), GROUP]),
                 )
 
         def turn_back(t):
-            for jb in range(4):
-                nc.tensor.transpose(banks[5 + t % 2][:, P * jb : P * (jb + 1)], turned[:, t, jb, :], ident[:])
+            for jb in range(S // P):
+                nc.tensor.transpose(
+                    banks[BACK_BANK + t % 2][:, P * jb : P * (jb + 1)], turned[:, t, jb, :], ident[:]
+                )
 
         def turn_fv():
-            nc.tensor.transpose(banks[5][:, 0:P], fv_rows[:], ident[:])
-            nc.scalar.copy(out=fv_cols[:], in_=banks[5][:, 0:4])
-            fourth = shared("fourth", [P, 4 * NP], BF16, "fourth", 1)
-            picked[3] = fourth[:, 0 : 2 * NP]
+            nc.tensor.transpose(banks[BACK_BANK][:, 0:P], fv_rows[:], ident[:])
+            nc.scalar.copy(out=fv_cols[:], in_=banks[BACK_BANK][:, 0:OUT_TILES])
+            tile3 = shared("tile3", [P, 4 * NP], BF16, "tile3")
+            picked[3] = tile3[:, 0 : 2 * NP]
             tanh_d[3] = picked[3].bitcast(F32)
-            tanh_b[3] = fourth[:, 2 * NP : 4 * NP].bitcast(F32)
-
-        def larger(u):
-            h[u] = shared(f"h{u}", [P, S], F32, row_tag(u - 1), 1)[:]
-            nc.vector.tensor_tensor(out=h[u], in0=tanh_b[u], in1=tanh_d[u], op=ALU.max)
+            tanh_b[3] = tile3[:, 2 * NP :].bitcast(F32)
 
         def scatter(u):
-            nc.vector.tensor_tensor(
-                out=pages[u][:].indirect(idx2[:]), in0=h[u], in1=gw[u][:], op=ALU.mult
-            )
+            nc.vector.tensor_tensor(out=pages[u][:].indirect(idx2[:]), in0=h[u], in1=gw[u][:], op=ALU.mult)
 
         def size(u):
-            return moved_rows[2] if u == 5 else picked[u + 1].bitcast(F32)
+            return size_after_weave if u == LAST - 2 else picked[u + 1].bitcast(F32)
 
-        def magnitude(u):
-            nc.scalar.activation(out=size(u), in_=fetched, func=ACT.Abs)
+        def dv_col(u):
+            return vec_cols[:, HALF + u : HALF + u + 1]
 
         def finish_x2(u):
-            nc.scalar.activation(out=picked[u][:, NP:], in_=size(u), func=ACT.Copy, scale=vec_cols[:, TILES + u : TILES + u + 1])
+            nc.scalar.activation(out=picked[u][:, NP:], in_=size(u), func=ACT.Copy, scale=dv_col(u))
             if u < HALF:
                 for t in range(PACK):
                     nc.sync.dma_start(
-                        out=moved[32 * u : 32 * (u + 1), t].rearrange("p x c -> p (x c)"), in_=picked[u][t:P:PACK]
+                        out=moved[QUAD_SIZE * u : QUAD_SIZE * (u + 1), t].rearrange("p x c -> p (x c)"),
+                        in_=picked[u][t:P:PACK],
                     )
 
-        moved_rows = [moved[:, t].rearrange("p x c -> p (x c)").bitcast(F32) for t in range(3)]
-        tanh_d[7], tanh_b[7] = moved_rows[0], moved_rows[1]
-        x_codes = {}
-        x_planes = {}
-
-        def weave(copy, dst, planes, cols):
-            count = planes.shape[1]
+        def weave(copy, dst, rows, cols):
             copy(
-                out=dst[:, cols, 0:count].rearrange("p (c i) j -> p c j i", i=4),
-                in_=planes[:, :, cols].rearrange("p j (c i) -> p c j i", i=4),
+                out=dst[:, cols, 0 : rows.shape[1]].rearrange("p (c i) j -> p c j i", i=LINE),
+                in_=rows[:, :, cols].rearrange("p j (c i) -> p c j i", i=LINE),
             )
+
+        x_codes, x_planes = {}, {}
 
         def quantise_x(half, which, cols, src):
             key = (half, which)
             if key not in x_codes:
-                tag, bufs = (("page5", "row6")[which], 1) if half == 0 else ("small", 6)
+                tag, bufs = (("page5", "row6")[which], 1) if half == 0 else ("small", SMALL_BUFS)
                 x_codes[key] = shared(f"x_codes{half}{which}", [P, NP], U32, tag, bufs)
                 x_planes[key] = held(f"x_planes{half}{which}", [P, NP], U8)
             nc.vector.quantize_mx(
                 out=x_codes[key][:, cols].bitcast(FP8X4), scales=x_planes[key][:, cols],
-                in_=src[:, cols, :].rearrange("p c j -> p (c j)"),
+                in_=src.rearrange("p c j -> p (c j)"),
             )
 
-        def second_stage(half, mt):
-            cols = slice(P * mt, P * (mt + 1))
-            nc.tensor.matmul_mx(
-                out=banks[4 + mt][:], lhsT=x_codes[half, 0][:, cols].bitcast(FP8X4), lhsT_scale=x_planes[half, 0][:, cols],
-                rhs=x_codes[half, 1][:].bitcast(FP8X4), rhs_scale=x_planes[half, 1][:],
-                start=(half == 0), stop=(half == 1),
-            )
+        def second_stage(half):
+            for mt in range(OUT_TILES):
+                cols = slice(P * mt, P * (mt + 1))
+                nc.tensor.matmul_mx(
+                    out=banks[E_BANK + mt][:],
+                    lhsT=x_codes[half, X1][:, cols].bitcast(FP8X4), lhsT_scale=x_planes[half, X1][:, cols],
+                    rhs=x_codes[half, X2][:].bitcast(FP8X4), rhs_scale=x_planes[half, X2][:],
+                    start=(half == 0), stop=(half == 1),
+                )
 
         cast(0, nc.scalar.copy)
         for a in range(PASSES):
@@ -325,86 +365,88 @@ def tile_list_braze_wetting_scores_kernel(
         squash(0)
         larger(0)
         cast(2, nc.scalar.copy)
-        turned = shared("wgs_turned", [P, PACK, 4, P], F32, "raw210", 1)
+        turned = shared("wgs_turned", [P, PACK, S // P, P], F32, "stage_main")
         gained_factor(1)
         squash(1)
-        nc.tensor.transpose(banks[4][:, 0:P], vec_rows[:], ident[:])
-        nc.scalar.copy(out=vec_cols[:], in_=banks[4][:, 0:16])
+        nc.tensor.transpose(banks[TURN_BANK][:, 0:P], vec_rows[:], ident[:])
+        nc.scalar.copy(out=vec_cols[:], in_=banks[TURN_BANK][:, 0 : HALF + TILES])
         nc.vector.tensor_copy(
             out=w4_dealt[:].bitcast(I32).rearrange("p a (t q w) -> p a t q w", t=PACK, w=4),
             in_=w4_halves[1][:].bitcast(I32).rearrange("p a (q t w) -> p a t q w", t=PACK, w=4),
         )
-        halves = (slice(0, 256), slice(256, 512))
+        everything = slice(0, NP)
+        halves = (slice(0, NP // 2), slice(NP // 2, NP))
 
-        for u in range(TILES):
+        for u in range(LAST):
             scatter(u)
             if u + 2 < TILES:
                 quantise_weights(u + 2)
                 first_stage(u + 2)
-            elif u + 1 < TILES:
-                quantise_x(0, 0, slice(0, NP), woven[0, 0])
-            if u + 1 == TILES:
-                continue
+            else:
+                quantise_x(0, X1, everything, woven[0, X1][:])
             nc.vector.tensor_copy(out=fetched, in_=pages[u][:].indirect(idx4[:]))
             larger(u + 1)
             if u + 3 < TILES:
                 cast(u + 3, nc.scalar.copy)
             nc.vector.tensor_copy(out=picked[u][:, 0:NP], in_=pages[u][:].indirect(idx3[:]))
-            if u == 5:
-                for which in range(2):
+            if u + 3 == TILES:
+                for which in (X1, X2):
                     for cols in halves:
                         weave(nc.scalar.copy, woven[0, which], moved[:, :, which, :], cols)
-            if u == 1:
+            if u + 3 == HALF:
                 turn_fv()
-            magnitude(u)
+            nc.scalar.activation(out=size(u), in_=fetched, func=ACT.Abs)
             if u + 2 < TILES:
                 squash(u + 2)
             finish_x2(u)
             if u == 0:
                 gained_factor(2)
                 gained_factor(3)
-                turn_wgs()
-            if u == 1:
-                w4_planes_dealt = shared("w4_planes_dealt", [P, PASSES, 512], U8, "row0", 1)
+            if u + 3 == HALF:
+                w4_planes_dealt = shared("w4_planes_dealt", [P, PASSES, H // 2], U8, "row0")
                 nc.vector.tensor_copy(
                     out=w4_planes_dealt[:].bitcast(I32).rearrange("p a (t q w) -> p a t q w", t=PACK, w=2),
                     in_=w4_planes[1][:].bitcast(I32).rearrange("p a (q t w) -> p a t q w", t=PACK, w=2),
                 )
-            if 2 <= u < 6:
-                gained_factor(u + 2)
-            if u == 1:
+                turn_wgs()
                 turn_back(0)
                 turn_back(1)
-            if 2 <= u < 4:
-                turn_back(u)
+            if HALF <= u + 2 < TILES:
+                gained_factor(u + 2)
+                if u < PACK:
+                    turn_back(u)
 
-        last = TILES - 1
-        planes_last = planes1[:].rearrange("p (t x) -> p t x", t=PACK)
-        last_x2 = shared("last_x2", [P, NP], F32, "small", 6)
-        weave(nc.scalar.copy, woven[1, 1], planes_last[:, 0:3, NP:], slice(0, NP))
+        scatter(LAST)
+        dealt_rows = dealt_x[:].rearrange("p (t x) -> p t x", t=PACK)
+        last_x2 = shared("last_x2", [P, NP], F32, "small", SMALL_BUFS)
+        weave(nc.scalar.copy, woven[1, X2], dealt_rows[:, 0 : PACK - 1, NP:], everything)
         for n, cols in enumerate(halves):
-            nc.vector.tensor_copy(out=last_x2[:, cols], in_=pages[last][:].indirect(idx4[:, 16 * n : 16 * (n + 1)]))
+            entries = idx4[:, 16 * n : 16 * (n + 1)]
+            nc.vector.tensor_copy(out=last_x2[:, cols], in_=pages[LAST][:].indirect(entries))
             last_size = picked[HALF + n][:, NP:].bitcast(F32)
             nc.scalar.activation(out=last_size, in_=last_x2[:, cols], func=ACT.Abs)
             nc.scalar.activation(
-                out=woven[1, 1][:, cols, 3], in_=last_size, func=ACT.Copy, scale=vec_cols[:, TILES + last : TILES + last + 1]
+                out=woven[1, X2][:, cols, PACK - 1], in_=last_size, func=ACT.Copy, scale=dv_col(LAST)
             )
-        quantise_x(0, 1, slice(0, NP), woven[0, 1])
-        for mt in range(4):
-            second_stage(0, mt)
+        quantise_x(0, X2, everything, woven[0, X2][:])
+        second_stage(0)
         for n, cols in enumerate(halves):
-            nc.vector.tensor_copy(out=picked[last][:, cols], in_=pages[last][:].indirect(idx3[:, 16 * n : 16 * (n + 1)]))
-        weave(nc.vector.tensor_copy, woven[1, 0], planes_last[:, :, 0:NP], halves[0])
-        quantise_x(1, 1, slice(0, NP), woven[1, 1])
-        quantise_x(1, 0, halves[0], woven[1, 0])
-        weave(nc.scalar.copy, woven[1, 0], planes_last[:, :, 0:NP], halves[1])
-        quantise_x(1, 0, halves[1], woven[1, 0])
-        for mt in range(4):
-            second_stage(1, mt)
-        for mt in range(4):
-            result = shared(f"result{mt}", [P, NP], F32, *(("woven10", 1) if mt == 0 else ("small", 6)))
+            entries = idx3[:, 16 * n : 16 * (n + 1)]
+            nc.vector.tensor_copy(out=picked[LAST][:, cols], in_=pages[LAST][:].indirect(entries))
+        weave(nc.vector.tensor_copy, woven[1, X1], dealt_rows[:, :, 0:NP], halves[0])
+        quantise_x(1, X2, everything, woven[1, X2][:])
+        quantise_x(1, X1, halves[0], woven[1, X1][:])
+        for mt in range(OUT_TILES // 2, OUT_TILES):
+            cols = slice(P * mt, P * (mt + 1))
+            spare = picked[HALF + OUT_TILES - 1 - mt][:, NP:].rearrange("p (c j) -> p c j", j=PACK)
+            weave(nc.scalar.copy, spare, dealt_rows[:, :, cols], slice(0, P))
+            quantise_x(1, X1, cols, spare)
+        second_stage(1)
+        for mt in range(OUT_TILES):
+            tag, bufs = ("dealt_x", 1) if mt == 0 else ("small", SMALL_BUFS)
+            result = shared(f"result{mt}", [P, NP], F32, tag, bufs)
             nc.vector.scalar_tensor_tensor(
-                out=result[:], in0=banks[4 + mt][:], scalar=fv_cols[:, mt : mt + 1], in1=jv_all[:],
+                out=result[:], in0=banks[E_BANK + mt][:], scalar=fv_cols[:, mt : mt + 1], in1=jv_all[:],
                 op0=ALU.add, op1=ALU.mult,
             )
             nc.sync.dma_start(out=out[P * mt : P * (mt + 1), :], in_=result[:])

from contextlib import ExitStack

import concourse.mybir as mybir
from concourse.masks import make_identity

K, T, S, H, T2, NP = 1024, 2048, 512, 1024, 1024, 512
FLOPS = 2 * (3 * K * H * S + H * NP * NP)

F32 = mybir.dt.float32
BF16 = mybir.dt.bfloat16
I32 = mybir.dt.int32
U32 = mybir.dt.uint32
U16 = mybir.dt.uint16
U8 = mybir.dt.uint8
FP8X4 = mybir.dt.float8_e4m3fn_x4
FP4X4 = mybir.dt.float4_e2m1fn_x4
ALU = mybir.AluOpType
ACT = mybir.ActivationFunctionType

P = 128
PACK = 4
SPAN = P * PACK
PASSES = K // SPAN
GROUP = 8
QUADS = 4
QUAD_SIZE = P // QUADS
SCALE_ROWS = QUAD_SIZE // GROUP
TILES = H // P
HALF = TILES // 2
LAST = TILES - 1
OUT_TILES = NP // P
LINE = 4
W1, W3 = 0, 1
PIECES = ((W3, 0), (W3, 1), (W1, 0), (W1, 1))
X1, X2 = 0, 1
SMALL_BUFS = 6
PLANE_RING = 3
CODES_LAG = 3
BANK_COLS = 512
E_BANK = 4
TURN_BANK, BACK_BANK, GAIN_BANK = 4, 5, 6


def tile_list_braze_wetting_scores_kernel(
    tc, tab_words, tab_scales, offs, w4_words, w4_scales, w1, w3, gain, page0, wgs, offs2, offs3, offs4, dv, fv, jv, out
):
    nc = tc.nc
    with ExitStack() as ctx:
        lists = ctx.enter_context(tc.tile_pool(name="lists", bufs=1))
        keep = ctx.enter_context(tc.tile_pool(name="keep", bufs=1))
        psum = ctx.enter_context(tc.psum_pool(name="psum", bufs=1))

        def held(name, shape, dtype):
            return keep.tile(shape, dtype, name=name, align_bytes=64)

        def shared(name, shape, dtype, tag, bufs=1):
            return keep.tile(shape, dtype, name=name, tag=tag, bufs=bufs, align_bytes=64)

        def piece_tag(u, w, a):
            return f"raw{u}{w}{a}"

        banks = [psum.tile([P, BANK_COLS], F32, name=f"bank{n}") for n in range(8)]
        weights = {W1: w1, W3: w3}

        tab_planes = held("tab_planes", [P, PASSES, T], U8)
        w4_planes = [held(f"w4_planes{n}", [P, PASSES, H // 2], U8) for n in range(2)]
        gain_rows = held("gain_rows", [P, P], F32)
        vec_rows = held("vec_rows", [P, P], F32)
        fv_rows = shared("fv_rows", [P, P], F32, "tile3")
        vec_cols = held("vec_cols", [P, HALF + TILES], F32)
        fv_cols = held("fv_cols", [P, OUT_TILES], F32)
        nc.vector.memset(tab_planes[:, 0, :].bitcast(I32), 0)
        nc.gpsimd.memset(tab_planes[:, 1, :].bitcast(I32), 0)
        nc.vector.memset(gain_rows[:], 0.0)
        for planes in w4_planes:
            nc.vector.memset(planes[:].bitcast(I32), 0)
        nc.vector.memset(vec_rows[:], 0.0)
        nc.vector.memset(fv_rows[:], 0.0)

        idx = lists.tile([P, S // 16], U16, name="idx")
        idx2 = lists.tile([P, S // 16], U16, name="idx2")
        idx3 = lists.tile([P, NP // 16], U16, name="idx3")
        idx4 = lists.tile([P, NP // 16], U16, name="idx4")

        raw, wide, pages = {}, {}, {}

        def load_natural_weights(u, pieces=PIECES):
            for w, a in pieces:
                handed_on = u >= 2 or (w, a) == PIECES[-1]
                tag, bufs = (piece_tag(u, w, a), 1) if handed_on else ("small", SMALL_BUFS)
                raw[u, w, a] = shared(f"raw{u}{w}{a}", [P, PACK, P], F32, tag, bufs)
                rows = weights[w][SPAN * a : SPAN * (a + 1), P * u : P * (u + 1)]
                nc.sync.dma_start(out=raw[u, w, a][:], in_=rows.rearrange("(p j) c -> p j c", j=PACK))

        def load_wide(w, a):
            wide[w, a] = held(f"wide{w}{a}", [P, PACK, H // 2], F32)
            rows = weights[w][SPAN * a : SPAN * (a + 1), H // 2 :]
            nc.sync.dma_start(out=wide[w, a][:], in_=rows.rearrange("(p j) c -> p j c", j=PACK))

        def load_page(u):
            pages[u] = shared(f"page{u}", [P, T2], F32, f"page{u}")
            if u < HALF:
                nc.sync.dma_start(out=pages[u][:], in_=page0[P * u : P * (u + 1), :])
            else:
                rows = page0[H // 2 :, :].rearrange("(q t i) c -> t q i c", t=PACK, i=GROUP)
                nc.sync.dma_start(out=pages[u][:], in_=rows[u - HALF])

        def load_scales(planes, src):
            for quad in range(QUADS):
                nc.sync.dma_start(
                    out=planes[QUAD_SIZE * quad : QUAD_SIZE * quad + SCALE_ROWS].bitcast(I32),
                    in_=src[:, SCALE_ROWS * quad : SCALE_ROWS * (quad + 1), :].rearrange("a r c -> r a c").bitcast(I32),
                )

        nc.sync.dma_start(idx[:], offs)
        tab = [shared(f"tab{a}", [P, T], U32, "large", PASSES) for a in range(PASSES)]

        def load_table(a):
            nc.sync.dma_start(out=tab[a][:].bitcast(I32), in_=tab_words[a].rearrange("p t i -> p (t i)").bitcast(I32))

        w4_halves = [held(f"w4_half{n}", [P, PASSES, H], U8) for n in range(2)]

        def load_w4(n):
            src = w4_words[:, :, H * n : H * (n + 1)].rearrange("a p c -> p a c")
            nc.sync.dma_start(out=w4_halves[n][:].bitcast(I32), in_=src.bitcast(I32))

        ident = held("ident", [P, P], F32)
        make_identity(nc, ident[:])
        wgs_nat = held("wgs_nat", [P, S], F32)
        load_natural_weights(0, PIECES[:2])
        load_scales(tab_planes, tab_scales)
        load_table(0)
        nc.sync.dma_start(out=gain_rows[0:HALF, :], in_=gain[0 : H // 2].rearrange("(u p) -> u p", p=P))
        load_natural_weights(0, PIECES[2:])
        load_table(1)
        load_w4(0)
        load_scales(w4_planes[0], w4_scales[:, :, 0 : H // 2])
        load_natural_weights(1)
        nc.sync.dma_start(out=wgs_nat[:], in_=wgs)
        nc.tensor.transpose(banks[GAIN_BANK][:, 0:P], gain_rows[:], ident[:])
        gain_first = shared("gain_first", [P, HALF], F32, piece_tag(0, *PIECES[-1]))
        nc.scalar.copy(out=gain_first[:], in_=banks[GAIN_BANK][:, 0:HALF])
        load_page(0)
        nc.sync.dma_start(idx2[:], offs2)
        nc.sync.dma_start(idx4[:], offs4)
        nc.sync.dma_start(idx3[:], offs3)
        load_natural_weights(2)
        nc.sync.dma_start(out=vec_rows[HALF:TILES, :], in_=dv[0 : H // 2].rearrange("(u p) -> u p", p=P))
        for row, vec in ((0, gain), (TILES, dv)):
            nc.sync.dma_start(
                out=vec_rows[row : row + HALF, :].rearrange("t (q i) -> t q i", i=GROUP),
                in_=vec[H // 2 :].rearrange("(q t i) -> t q i", t=PACK, i=GROUP),
            )
        load_natural_weights(3, PIECES[:1])
        load_page(1)
        load_natural_weights(3, PIECES[1:])
        load_scales(w4_planes[1], w4_scales[:, :, H // 2 :])
        for n, (w, a) in enumerate(PIECES):
            load_wide(w, a)
            if n == 1:
                load_page(2)
        nc.sync.dma_start(out=fv_rows[0:OUT_TILES, :], in_=fv.rearrange("(u p) -> u p", p=P))
        load_w4(1)
        for u in range(3, TILES):
            load_page(u)
        jv_all = held("jv_all", [P, NP], F32)
        nc.sync.dma_start(out=jv_all[:], in_=jv.partition_broadcast(P))

        v_scales = [held(f"v_scales{a}", [P, S], U8) for a in range(PASSES)]
        v_words = [held(f"v_words{a}", [P, S], U32) for a in range(PASSES)]

        stage_main = shared("stage_main", [P, len(PIECES) * SPAN], BF16, "stage_main")
        stage_second = held("stage_second", [P, len(PIECES) * SPAN], BF16)
        stage_dealt = held("stage_dealt", [P, len(PIECES) * SPAN], BF16)
        stage = [stage_main[:], stage_second[:], stage_main[:], stage_main[:]] + [stage_dealt[:]] * HALF
        w_codes, gw, h = {}, {}, {}
        w_planes = [held(f"w_planes{n}", [P, len(PIECES) * P], U8) for n in range(PLANE_RING)]
        tanh_d = [None] * TILES
        tanh_b = [held(f"tanh_b{n}", [P, S], F32)[:] for n in range(2)] * HALF
        after = {u: shared(f"after{u}", [P, 3 * S], F32, piece_tag(u, *PIECES[-1])) for u in (2, 3)}
        for u in (1, 2):
            tanh_d[u], tanh_b[u] = after[u + 1][:, 0:S], after[u + 1][:, S : 2 * S]
        fetched = after[2][:, 2 * S :]
        tanh_d[0] = shared("tanh_d_first", [P, S], F32, "row1")[:]

        def row_tag(u):
            taken_over = {
                -1: piece_tag(1, *PIECES[-1]),
                2: piece_tag(3, *PIECES[1]),
                3: piece_tag(3, *PIECES[2]),
                5: f"page{4 - CODES_LAG}",
                7: f"page{6 - CODES_LAG}",
            }
            return taken_over.get(u, f"row{u}")

        w4_dealt = held("w4_dealt", [P, PASSES, H], U8)
        woven = {
            (half, which): held(f"woven{half}{which}", [P, NP // 2 if (half, which) == (1, X1) else NP, PACK], BF16)
            for half in range(2)
            for which in (X1, X2)
        }
        moved = shared("moved", [P, PACK, 2, NP], BF16, "large", PASSES)
        dealt_x = shared("dealt_x", [P, PACK * 2 * NP], BF16, "dealt_x")
        picked = [
            raw[3, W3, 0][:].rearrange("p j c -> p (j c)").bitcast(BF16),
            after[3][:, 2 * S :].bitcast(BF16),
            tanh_d[2].bitcast(BF16),
            None,
        ] + [dealt_x[:, 2 * NP * t : 2 * NP * (t + 1)] for t in range(PACK)]
        for u in range(HALF, LAST):
            tanh_d[u] = picked[u].bitcast(F32)
        moved_rows = [moved[:, t].rearrange("p x c -> p (x c)").bitcast(F32) for t in range(3)]
        tanh_d[LAST], tanh_b[LAST], size_after_weave = moved_rows

        def cast(u, copy):
            for w, a in PIECES:
                n = PASSES * w + a
                dst = stage[u][:, SPAN * n : SPAN * (n + 1)]
                if u < HALF:
                    copy(
                        out=dst.rearrange("p (c i j) -> p c j i", i=LINE, j=PACK),
                        in_=raw[u, w, a][:].rearrange("p j (c i) -> p c j i", i=LINE),
                    )
                else:
                    src = wide[w, a][:].rearrange("p j (q t g i) -> p t q g j i", t=PACK, g=GROUP // LINE, i=LINE)
                    copy(
                        out=dst.rearrange("p (q g i j) -> p q g j i", g=GROUP // LINE, i=LINE, j=PACK),
                        in_=src[:, u - HALF],
                    )

        def quantise_weights(u):
            if u < CODES_LAG:
                w_codes[u] = held(f"w_codes{u}", [P, len(PIECES) * P], U32)
            else:
                w_codes[u] = shared(f"w_codes{u}", [P, len(PIECES) * P], U32, f"page{u - CODES_LAG}")
            nc.vector.quantize_mx(out=w_codes[u][:].bitcast(FP8X4), scales=w_planes[u % PLANE_RING][:], in_=stage[u])

        def b_bank(u):
            return banks[2 * (u % 2)]

        def d_bank(u):
            return banks[2 * (u % 2) + 1]

        def first_stage(u):
            def product(bank, lhs, lhs_scale, a, start, stop):
                nc.tensor.matmul_mx(
                    out=bank[:], lhsT=lhs, lhsT_scale=lhs_scale, rhs=v_words[a][:].bitcast(FP8X4),
                    rhs_scale=v_scales[a][:], start=start, stop=stop,
                )

            def fp8(w, a):
                cols = slice(P * (PASSES * w + a), P * (PASSES * w + a + 1))
                return w_codes[u][:, cols].bitcast(FP8X4), w_planes[u % PLANE_RING][:, cols]

            def fp4(a):
                words, scales = (w4_halves[0], w4_planes[0]) if u < HALF else (w4_dealt, w4_planes_dealt)
                c = u % HALF
                return words[:, a, 2 * P * c : 2 * P * (c + 1)].bitcast(FP4X4), scales[:, a, P * c : P * (c + 1)]

            for a in range(PASSES):
                first, final = a == 0, a == PASSES - 1
                product(d_bank(u), *fp8(W3, a), a, first, final)
                product(b_bank(u), *fp8(W1, a), a, first, False)
                product(b_bank(u), *fp4(a), a, False, final)

        def squash(u):
            nc.scalar.activation(out=tanh_d[u], in_=d_bank(u)[:], func=ACT.Tanh)
            nc.scalar.activation(out=tanh_b[u], in_=b_bank(u)[:], func=ACT.Tanh)

        def larger(u):
            h[u] = shared(f"h{u}", [P, S], F32, row_tag(u - 1))[:]
            nc.vector.tensor_tensor(out=h[u], in0=tanh_b[u], in1=tanh_d[u], op=ALU.max)

        def gained_factor(u):
            if u < HALF:
                factor, gains = wgs_nat[:], gain_first[:, u : u + 1]
            else:
                factor, gains = banks[BACK_BANK + u % 2][:], vec_cols[:, u - HALF : u - HALF + 1]
            gw[u] = shared(f"gw{u}", [P, S], F32, row_tag(u))
            nc.scalar.activation(out=gw[u][:], in_=factor, func=ACT.Copy, scale=gains)

        def turn_wgs():
            for jb in range(S // P):
                cols = slice(P * jb, P * (jb + 1))
                nc.tensor.transpose(banks[TURN_BANK][:, cols], wgs_nat[:, cols], ident[:])
            for t in range(PACK):
                src = banks[TURN_BANK][:].rearrange("p (b q t i) -> p t b q i", b=S // P, t=PACK, i=GROUP)[:, t]
                nc.scalar.copy(
                    out=turned[:, t].rearrange("p b (g q i) -> p b g q i", g=QUADS, i=GROUP),
                    in_=src.unsqueeze(2).to_broadcast([P, S // P, QUADS, P // (PACK * GROUP), GROUP]),
                )

        def turn_back(t):
            for jb in range(S // P):
                nc.tensor.transpose(
                    banks[BACK_BANK + t % 2][:, P * jb : P * (jb + 1)], turned[:, t, jb, :], ident[:]
                )

        def turn_fv():
            nc.tensor.transpose(banks[BACK_BANK][:, 0:P], fv_rows[:], ident[:])
            nc.scalar.copy(out=fv_cols[:], in_=banks[BACK_BANK][:, 0:OUT_TILES])
            tile3 = shared("tile3", [P, 4 * NP], BF16, "tile3")
            picked[3] = tile3[:, 0 : 2 * NP]
            tanh_d[3] = picked[3].bitcast(F32)
            tanh_b[3] = tile3[:, 2 * NP :].bitcast(F32)

        def scatter(u):
            nc.vector.tensor_tensor(out=pages[u][:].indirect(idx2[:]), in0=h[u], in1=gw[u][:], op=ALU.mult)

        def size(u):
            return size_after_weave if u == LAST - 2 else picked[u + 1].bitcast(F32)

        def dv_col(u):
            return vec_cols[:, HALF + u : HALF + u + 1]

        def finish_x2(u):
            nc.scalar.activation(out=picked[u][:, NP:], in_=size(u), func=ACT.Copy, scale=dv_col(u))
            if u < HALF:
                for t in range(PACK):
                    nc.sync.dma_start(
                        out=moved[QUAD_SIZE * u : QUAD_SIZE * (u + 1), t].rearrange("p x c -> p (x c)"),
                        in_=picked[u][t:P:PACK],
                    )

        def weave(copy, dst, rows, cols):
            copy(
                out=dst[:, cols, 0 : rows.shape[1]].rearrange("p (c i) j -> p c j i", i=LINE),
                in_=rows[:, :, cols].rearrange("p j (c i) -> p c j i", i=LINE),
            )

        x_codes, x_planes = {}, {}

        def quantise_x(half, which, cols, src):
            key = (half, which)
            if key not in x_codes:
                tag, bufs = (("page5", "row6")[which], 1) if half == 0 else ("small", SMALL_BUFS)
                x_codes[key] = shared(f"x_codes{half}{which}", [P, NP], U32, tag, bufs)
                x_planes[key] = held(f"x_planes{half}{which}", [P, NP], U8)
            nc.vector.quantize_mx(
                out=x_codes[key][:, cols].bitcast(FP8X4), scales=x_planes[key][:, cols],
                in_=src.rearrange("p c j -> p (c j)"),
            )

        def second_stage(half):
            for mt in range(OUT_TILES):
                cols = slice(P * mt, P * (mt + 1))
                nc.tensor.matmul_mx(
                    out=banks[E_BANK + mt][:],
                    lhsT=x_codes[half, X1][:, cols].bitcast(FP8X4), lhsT_scale=x_planes[half, X1][:, cols],
                    rhs=x_codes[half, X2][:].bitcast(FP8X4), rhs_scale=x_planes[half, X2][:],
                    start=(half == 0), stop=(half == 1),
                )

        cast(0, nc.scalar.copy)
        for a in range(PASSES):
            nc.vector.tensor_copy(out=v_scales[a][:], in_=tab_planes[:, a, :].indirect(idx[:]))
            nc.vector.tensor_copy(out=v_words[a][:], in_=tab[a][:].indirect(idx[:]))
            if a == 0:
                quantise_weights(0)
        first_stage(0)
        cast(1, nc.vector.tensor_copy)
        quantise_weights(1)
        first_stage(1)
        gained_factor(0)
        squash(0)
        larger(0)
        cast(2, nc.scalar.copy)
        turned = shared("wgs_turned", [P, PACK, S // P, P], F32, "stage_main")
        gained_factor(1)
        squash(1)
        nc.tensor.transpose(banks[TURN_BANK][:, 0:P], vec_rows[:], ident[:])
        nc.scalar.copy(out=vec_cols[:], in_=banks[TURN_BANK][:, 0 : HALF + TILES])
        nc.vector.tensor_copy(
            out=w4_dealt[:].bitcast(I32).rearrange("p a (t q w) -> p a t q w", t=PACK, w=4),
            in_=w4_halves[1][:].bitcast(I32).rearrange("p a (q t w) -> p a t q w", t=PACK, w=4),
        )
        everything = slice(0, NP)
        halves = (slice(0, NP // 2), slice(NP // 2, NP))

        for u in range(LAST):
            scatter(u)
            if u + 2 < TILES:
                quantise_weights(u + 2)
                first_stage(u + 2)
            else:
                quantise_x(0, X1, everything, woven[0, X1][:])
            nc.vector.tensor_copy(out=fetched, in_=pages[u][:].indirect(idx4[:]))
            larger(u + 1)
            if u + 3 < TILES:
                cast(u + 3, nc.scalar.copy)
            nc.vector.tensor_copy(out=picked[u][:, 0:NP], in_=pages[u][:].indirect(idx3[:]))
            if u + 3 == TILES:
                for which in (X1, X2):
                    for cols in halves:
                        weave(nc.scalar.copy, woven[0, which], moved[:, :, which, :], cols)
            if u + 3 == HALF:
                turn_fv()
            nc.scalar.activation(out=size(u), in_=fetched, func=ACT.Abs)
            if u + 2 < TILES:
                squash(u + 2)
            finish_x2(u)
            if u == 0:
                gained_factor(2)
                gained_factor(3)
            if u + 3 == HALF:
                w4_planes_dealt = shared("w4_planes_dealt", [P, PASSES, H // 2], U8, "row0")
                nc.vector.tensor_copy(
                    out=w4_planes_dealt[:].bitcast(I32).rearrange("p a (t q w) -> p a t q w", t=PACK, w=2),
                    in_=w4_planes[1][:].bitcast(I32).rearrange("p a (q t w) -> p a t q w", t=PACK, w=2),
                )
                turn_wgs()
                turn_back(0)
                turn_back(1)
            if HALF <= u + 2 < TILES:
                gained_factor(u + 2)
                if u < PACK:
                    turn_back(u)

        scatter(LAST)
        dealt_rows = dealt_x[:].rearrange("p (t x) -> p t x", t=PACK)
        last_x2 = shared("last_x2", [P, NP], F32, "small", SMALL_BUFS)
        weave(nc.scalar.copy, woven[1, X2], dealt_rows[:, 0 : PACK - 1, NP:], everything)
        for n, cols in enumerate(halves):
            entries = idx4[:, 16 * n : 16 * (n + 1)]
            nc.vector.tensor_copy(out=last_x2[:, cols], in_=pages[LAST][:].indirect(entries))
            last_size = picked[HALF + n][:, NP:].bitcast(F32)
            nc.scalar.activation(out=last_size, in_=last_x2[:, cols], func=ACT.Abs)
            nc.scalar.activation(
                out=woven[1, X2][:, cols, PACK - 1], in_=last_size, func=ACT.Copy, scale=dv_col(LAST)
            )
        quantise_x(0, X2, everything, woven[0, X2][:])
        second_stage(0)
        for n, cols in enumerate(halves):
            entries = idx3[:, 16 * n : 16 * (n + 1)]
            nc.vector.tensor_copy(out=picked[LAST][:, cols], in_=pages[LAST][:].indirect(entries))
        weave(nc.vector.tensor_copy, woven[1, X1], dealt_rows[:, :, 0:NP], halves[0])
        quantise_x(1, X2, everything, woven[1, X2][:])
        quantise_x(1, X1, halves[0], woven[1, X1][:])
        for mt in range(OUT_TILES // 2, OUT_TILES):
            cols = slice(P * mt, P * (mt + 1))
            spare = picked[HALF + OUT_TILES - 1 - mt][:, NP:].rearrange("p (c j) -> p c j", j=PACK)
            weave(nc.scalar.copy, spare, dealt_rows[:, :, cols], slice(0, P))
            quantise_x(1, X1, cols, spare)
        second_stage(1)
        for mt in range(OUT_TILES):
            tag, bufs = ("dealt_x", 1) if mt == 0 else ("small", SMALL_BUFS)
            result = shared(f"result{mt}", [P, NP], F32, tag, bufs)
            nc.vector.scalar_tensor_tensor(
                out=result[:], in0=banks[E_BANK + mt][:], scalar=fv_cols[:, mt : mt + 1], in1=jv_all[:],
                op0=ALU.add, op1=ALU.mult,
            )
            nc.sync.dma_start(out=out[P * mt : P * (mt + 1), :], in_=result[:])
